import numpy as np
import ml_dtypes


def mxq(x, axis, fmt="e4m3"):
    dtype, down = {"e4m3": (ml_dtypes.float8_e4m3fn, 7), "e5m2": (ml_dtypes.float8_e5m2, 14)}[fmt]
    v = np.moveaxis(np.asarray(x, np.float32).astype(ml_dtypes.bfloat16).astype(np.float64), axis, -1)
    blocks = v.reshape(v.shape[:-1] + (-1, 32))
    amax = np.abs(blocks).max(-1, keepdims=True)
    byte = np.maximum(np.where(amax > 0, np.frexp(amax)[1] - 1 + 127, 0) - down, 1)
    scale = np.exp2(byte - 127.0)
    codes = (blocks / scale).astype(np.float32).astype(dtype).astype(np.float64)
    return np.moveaxis((codes * scale).reshape(v.shape), -1, axis)


WIDE = False


def mx_kscale(k):
    if not WIDE:
        return np.ones(k)
    levels = np.array([10, -10, 5, -5, 0])
    if k % 512:
        return np.exp2(np.random.permutation(np.resize(levels, k // 32))).repeat(32)
    a = np.empty((k // 512, 16))
    for p in range(k // 512):
        a[p, :8] = np.random.permutation(np.resize(levels, 8))
        for g in range(8):
            far = levels[np.abs(levels - a[p, g]) >= 10]
            a[p, g + 8] = far[np.random.randint(len(far))]
    return np.exp2(a.ravel()).repeat(32)


def f64(x):
    return np.asarray(x).astype(np.float64)


def striped(idx):
    return np.tile(idx.reshape(-1, 16).T, (8, 1)).astype(np.uint16)


def unstriped(offs):
    return offs[:16].T.reshape(-1).astype(np.int64)


K, T, E, C, N = 1024, 512, 4, 256, 512


def by_expert(wq, xq):
    return np.concatenate([wq[e].T @ xq[:, e * C:(e + 1) * C] for e in range(E)], axis=1)


def setup_inputs():
    n = np.random.standard_normal
    s = mx_kscale(K)[:, None]
    first = np.random.permutation(np.repeat(np.arange(E), T // E))
    second = (first + 1 + np.random.permutation(np.repeat(np.arange(E - 1), -(-T // (E - 1)))[:T])) % E
    while np.bincount(second, minlength=E).max() != T // E:
        load = np.bincount(second, minlength=E); hi, lo = int(load.argmax()), int(load.argmin())
        t = np.flatnonzero((second == hi) & (first != lo))[0]; second[t] = lo
    slot_token = np.empty(E * C, np.int64); pos = np.empty((2, T), np.int64); fill = np.zeros(E, np.int64)
    place = np.stack([np.random.permutation(C) for _ in range(E)])
    for r, deal in enumerate((first, second)):
        for t in np.random.permutation(T):
            e = deal[t]; j = e * C + place[e, fill[e]]; fill[e] += 1; slot_token[j] = t; pos[r, t] = j
    g = np.random.uniform(0.2, 0.8, T)
    return {
        "xT": (n((K, T)) * s).astype(np.float32),
        "w": (n((E, K, N)) / np.sqrt(K) / s[None]).astype(np.float32),
        "gate": np.stack([np.tile(g, (N, 1)), np.tile(1.0 - g, (N, 1))]).astype(np.float32),
        "offs": striped(slot_token),
        "pos1": striped(pos[0]),
        "pos2": striped(pos[1]),
    }


def reference(xT, w, gate, offs, pos1, pos2):
    idx = unstriped(offs)
    xq = mxq(f64(xT)[:, idx], 0, "e4m3")
    y = by_expert(mxq(f64(w), 1, "e4m3"), xq)
    return f64(gate[0]) * y[:, unstriped(pos1)] + f64(gate[1]) * y[:, unstriped(pos2)]

@@ -1,0 +1,209 @@
+from contextlib import ExitStack
+
+import concourse.mybir as mybir
+
+K, T, E, C, N = 1024, 512, 4, 256, 512
+FLOPS = 2 * K * N * E * C
+
+F32 = mybir.dt.float32
+BF16 = mybir.dt.bfloat16
+U32 = mybir.dt.uint32
+U16 = mybir.dt.uint16
+U8 = mybir.dt.uint8
+FP8X4 = mybir.dt.float8_e4m3fn_x4
+MULT = mybir.AluOpType.mult
+ADD = mybir.AluOpType.add
+
+P = 128
+PACK = 4
+K_PASS = P * PACK
+PASSES = K // K_PASS
+NB = N // P
+HALF = 2 * P
+
+TOKEN_ORDER = ((0, 0), (0, 1), (1, 0), (1, 1), (0, 2), (1, 2), (0, 3), (1, 3))
+
+
+def interleave(engine_copy, dst, src):
+    engine_copy(
+        out=dst.rearrange("p (c i) t -> p c t i", i=4),
+        in_=src.rearrange("p t (c i) -> p c t i", i=4),
+    )
+
+
+def tile_routed_moe_kernel(tc, xT, w, gate, offs, pos1, pos2, out):
+    nc = tc.nc
+    with ExitStack() as ctx:
+        lists = ctx.enter_context(tc.tile_pool(name="lists", bufs=1))
+        keep = ctx.enter_context(tc.tile_pool(name="keep", bufs=1))
+        gath = ctx.enter_context(tc.tile_pool(name="gath", bufs=4))
+        tgrp = ctx.enter_context(tc.tile_pool(name="tgrp", bufs=4))
+        wgh = ctx.enter_context(tc.tile_pool(name="wgh", bufs=4))
+        wgq = ctx.enter_context(tc.tile_pool(name="wgq", bufs=8))
+        comb = ctx.enter_context(tc.tile_pool(name="comb", bufs=2))
+        psum = ctx.enter_context(tc.psum_pool(name="psum", bufs=1))
+
+        offs_t = lists.tile([P, E * C // 16], U16, name="offs_t")
+        nc.sync.dma_start(offs_t[:], offs)
+        pos_t = [lists.tile([P, T // 16], U16, name="pos_t%d" % r) for r in range(2)]
+
+        warm_in = keep.tile([P, 8], F32, name="warm_in")
+        warm_out = keep.tile([P, 8], F32, name="warm_out")
+        nc.vector.memset(warm_in[:], 0.0)
+        nc.scalar.copy(out=warm_out[:], in_=warm_in[:])
+
+        x_view = xT.rearrange("(g p t) n -> g p t n", p=P, t=PACK)
+        planes = [[keep.tile([P, T], F32, name="x%d%d" % (g, t)) for t in range(PACK)] for g in range(PASSES)]
+        w_raw = [[keep.tile([P, PACK, N], F32, name="w%d%d" % (e, g)) for g in range(PASSES)] for e in range(E)]
+        gates = [[keep.tile([P, T], F32, name="gate%d%d" % (r, nb)) for nb in range(NB)] for r in range(2)]
+
+        def load_planes(g):
+            for t in range(PACK):
+                nc.sync.dma_start(planes[g][t][:], x_view[g, :, t, :])
+
+        def load_w(e, g):
+            nc.sync.dma_start(
+                w_raw[e][g][:],
+                w[e, g * K_PASS : (g + 1) * K_PASS, :].rearrange("(p j) n -> p j n", j=PACK),
+            )
+
+        load_planes(0)
+        load_w(0, 0)
+        load_planes(1)
+        nc.sync.dma_start(pos_t[0][:], pos1)
+        nc.sync.dma_start(pos_t[1][:], pos2)
+        for e in range(E):
+            for g in range(PASSES):
+                if (e, g) != (0, 0):
+                    load_w(e, g)
+        for nb in range(NB):
+            for r in range(2):
+                nc.sync.dma_start(gates[r][nb][:], gate[r, nb * P : (nb + 1) * P, :])
+
+        t_codes = keep.tile([P, PASSES, E * C], U32, name="t_codes", align_bytes=64)
+        t_scales = keep.tile([P, PASSES, E * C], U8, name="t_scales", align_bytes=64)
+        wa_codes = keep.tile([P, E, PASSES, HALF], U32, name="wa_codes", align_bytes=64)
+        wa_scales = keep.tile([P, E, PASSES, HALF], U8, name="wa_scales", align_bytes=64)
+        wb_codes = keep.tile([P, NB - 2, E, PASSES * P], U32, name="wb_codes", align_bytes=64)
+        wb_scales = keep.tile([P, NB - 2, E, PASSES * P], U8, name="wb_scales", align_bytes=64)
+        y = [keep.tile([P, E * C], F32, name="y%d" % nb) for nb in range(NB)]
+        banks = [[psum.tile([P, 2 * C], F32, name="ps%d%d" % (nb, pr)) for pr in range(E // 2)] for nb in range(NB)]
+
+        tok_done = set()
+        w_done = set()
+        mm_done = set()
+
+        def emit_matmuls():
+            for nb in range(NB):
+                for e in range(E):
+                    if (nb, e) in mm_done:
+                        continue
+                    if not all((g, e) in tok_done and (nb, e, g) in w_done for g in range(PASSES)):
+                        continue
+                    if e % 2 == 1 and (nb, e - 1) not in mm_done:
+                        continue
+                    bank = banks[nb][e // 2]
+                    for g in range(PASSES):
+                        if nb < 2:
+                            lhs_codes = wa_codes[:, e, g, nb * P : (nb + 1) * P]
+                            lhs_scales = wa_scales[:, e, g, nb * P : (nb + 1) * P]
+                        else:
+                            lhs_codes = wb_codes[:, nb - 2, e, g * P : (g + 1) * P]
+                            lhs_scales = wb_scales[:, nb - 2, e, g * P : (g + 1) * P]
+                        nc.tensor.matmul_mx(
+                            out=bank[:, (e % 2) * C : (e % 2 + 1) * C],
+                            lhsT=lhs_codes.bitcast(FP8X4),
+                            lhsT_scale=lhs_scales,
+                            rhs=t_codes[:, g, e * C : (e + 1) * C].bitcast(FP8X4),
+                            rhs_scale=t_scales[:, g, e * C : (e + 1) * C],
+                            start=(g == 0),
+                            stop=(g == PASSES - 1),
+                        )
+                    mm_done.add((nb, e))
+                    if e % 2 == 1:
+                        nc.scalar.copy(out=y[nb][:, (e - 1) * C : (e + 1) * C], in_=bank[:])
+
+        def token_gather(g, e):
+            g4 = gath.tile([P, PACK, C], F32, name="g4")
+            for t in range(PACK):
+                nc.vector.tensor_copy(g4[:, t, :], planes[g][t][:].indirect(offs_t[:, e * (C // 16) : (e + 1) * (C // 16)]))
+            grouped = tgrp.tile([P, C, PACK], BF16, name="tg", align_bytes=64)
+            interleave(nc.scalar.copy, grouped[:], g4[:])
+            return grouped
+
+        def token_quantize(g, e, grouped):
+            nc.vector.quantize_mx(
+                out=t_codes[:, g, e * C : (e + 1) * C].bitcast(FP8X4),
+                scales=t_scales[:, g, e * C : (e + 1) * C],
+                in_=grouped[:].rearrange("p c t -> p (c t)"),
+            )
+            tok_done.add((g, e))
+
+        def half_interleave(e, g):
+            grouped = wgh.tile([P, HALF, PACK], BF16, name="wg", align_bytes=64)
+            interleave(nc.scalar.copy, grouped[:], w_raw[e][g][:, :, 0:HALF])
+            return grouped
+
+        def half_quantize(e, g, grouped):
+            nc.vector.quantize_mx(
+                out=wa_codes[:, e, g, :].bitcast(FP8X4),
+                scales=wa_scales[:, e, g, :],
+                in_=grouped[:].rearrange("p c t -> p (c t)"),
+            )
+            w_done.add((0, e, g))
+            w_done.add((1, e, g))
+
+        def block_interleave(nb, e):
+            grouped = wgq.tile([P, PASSES, P, PACK], BF16, name="wg", align_bytes=64)
+            for g in range(PASSES):
+                interleave(nc.scalar.copy, grouped[:, g, :, :], w_raw[e][g][:, :, nb * P : (nb + 1) * P])
+            return grouped
+
+        def block_quantize(nb, e, grouped):
+            nc.vector.quantize_mx(
+                out=wb_codes[:, nb - 2, e, :].bitcast(FP8X4),
+                scales=wb_scales[:, nb - 2, e, :],
+                in_=grouped[:].rearrange("p g c t -> p (g c t)"),
+            )
+            for g in range(PASSES):
+                w_done.add((nb, e, g))
+
+        w_order = [(e, g) for e in range(E) for g in range(PASSES)]
+        pending = []
+        for i in range(len(TOKEN_ORDER)):
+            g, e = TOKEN_ORDER[i]
+            tg = token_gather(g, e)
+            we, wpass = w_order[i]
+            wgr = half_interleave(we, wpass)
+            for job in pending:
+                job()
+            emit_matmuls()
+            pending = [
+                lambda g=g, e=e, tg=tg: token_quantize(g, e, tg),
+                lambda we=we, wpass=wpass, wgr=wgr: half_quantize(we, wpass, wgr),
+            ]
+        for job in pending:
+            job()
+        emit_matmuls()
+
+        jobs = []
+        ran = 0
+        for nb in range(2, NB):
+            for e in range(E):
+                wgr = block_interleave(nb, e)
+                jobs.append(lambda e=e, nb=nb, wgr=wgr: block_quantize(nb, e, wgr))
+                if len(jobs) - ran > 1:
+                    jobs[ran]()
+                    ran += 1
+                    emit_matmuls()
+        for job in jobs[ran:]:
+            job()
+        emit_matmuls()
+
+        for nb in range(NB):
+            part = [comb.tile([P, T], F32, name="part%d" % r) for r in range(2)]
+            for r in range(2):
+                nc.vector.tensor_tensor(part[r][:], y[nb][:].indirect(pos_t[r][:]), gates[r][nb][:], MULT)
+            total = comb.tile([P, T], F32, name="total")
+            nc.vector.tensor_tensor(total[:], part[0][:], part[1][:], ADD)
+            nc.sync.dma_start(out[nb * P : (nb + 1) * P, :], total[:])

@@ -13,6 +13,7 @@ U8 = mybir.dt.uint8
 FP8X4 = mybir.dt.float8_e4m3fn_x4
 MULT = mybir.AluOpType.mult
 ADD = mybir.AluOpType.add
+COPY = mybir.ActivationFunctionType.Copy
 
 P = 128
 PACK = 4
@@ -20,15 +21,7 @@ K_PASS = P * PACK
 PASSES = K // K_PASS
 NB = N // P
 HALF = 2 * P
-
-TOKEN_ORDER = ((0, 0), (0, 1), (1, 0), (1, 1), (0, 2), (1, 2), (0, 3), (1, 3))
-
-
-def interleave(engine_copy, dst, src):
-    engine_copy(
-        out=dst.rearrange("p (c i) t -> p c t i", i=4),
-        in_=src.rearrange("p t (c i) -> p c t i", i=4),
-    )
+LC = C // 16
 
 
 def tile_routed_moe_kernel(tc, xT, w, gate, offs, pos1, pos2, out):
@@ -36,58 +29,65 @@ def tile_routed_moe_kernel(tc, xT, w, gate, offs, pos1, pos2, out):
     with ExitStack() as ctx:
         lists = ctx.enter_context(tc.tile_pool(name="lists", bufs=1))
         keep = ctx.enter_context(tc.tile_pool(name="keep", bufs=1))
-        gath = ctx.enter_context(tc.tile_pool(name="gath", bufs=4))
-        tgrp = ctx.enter_context(tc.tile_pool(name="tgrp", bufs=4))
-        wgh = ctx.enter_context(tc.tile_pool(name="wgh", bufs=4))
-        wgq = ctx.enter_context(tc.tile_pool(name="wgq", bufs=8))
-        comb = ctx.enter_context(tc.tile_pool(name="comb", bufs=2))
+        comb = ctx.enter_context(tc.tile_pool(name="comb", bufs=3))
         psum = ctx.enter_context(tc.psum_pool(name="psum", bufs=1))
 
         offs_t = lists.tile([P, E * C // 16], U16, name="offs_t")
-        nc.sync.dma_start(offs_t[:], offs)
         pos_t = [lists.tile([P, T // 16], U16, name="pos_t%d" % r) for r in range(2)]
-
         warm_in = keep.tile([P, 8], F32, name="warm_in")
         warm_out = keep.tile([P, 8], F32, name="warm_out")
-        nc.vector.memset(warm_in[:], 0.0)
-        nc.scalar.copy(out=warm_out[:], in_=warm_in[:])
-
-        x_view = xT.rearrange("(g p t) n -> g p t n", p=P, t=PACK)
-        planes = [[keep.tile([P, T], F32, name="x%d%d" % (g, t)) for t in range(PACK)] for g in range(PASSES)]
-        w_raw = [[keep.tile([P, PACK, N], F32, name="w%d%d" % (e, g)) for g in range(PASSES)] for e in range(E)]
-        gates = [[keep.tile([P, T], F32, name="gate%d%d" % (r, nb)) for nb in range(NB)] for r in range(2)]
-
-        def load_planes(g):
-            for t in range(PACK):
-                nc.sync.dma_start(planes[g][t][:], x_view[g, :, t, :])
-
-        def load_w(e, g):
-            nc.sync.dma_start(
-                w_raw[e][g][:],
-                w[e, g * K_PASS : (g + 1) * K_PASS, :].rearrange("(p j) n -> p j n", j=PACK),
-            )
-
-        load_planes(0)
-        load_w(0, 0)
-        load_planes(1)
-        nc.sync.dma_start(pos_t[0][:], pos1)
-        nc.sync.dma_start(pos_t[1][:], pos2)
-        for e in range(E):
-            for g in range(PASSES):
-                if (e, g) != (0, 0):
-                    load_w(e, g)
-        for nb in range(NB):
-            for r in range(2):
-                nc.sync.dma_start(gates[r][nb][:], gate[r, nb * P : (nb + 1) * P, :])
-
+        xf = [keep.tile([P, PACK, T], F32, name="xf%d" % g) for g in range(PASSES)]
+        xb = keep.tile([P, PACK, T], BF16, name="xb")
+        wh = [[keep.tile([P, PASSES, PACK, HALF], F32, name="wh%d%d" % (h, e)) for e in range(E)] for h in range(2)]
+        gt = [[keep.tile([P, 2, T], F32, name="gt%d%d" % (r, h)) for h in range(2)] for r in range(2)]
+        tg = [[keep.tile([P, C, PACK], BF16, name="tg%d%d" % (g, e), align_bytes=64) for e in range(E)] for g in range(PASSES)]
+        wg = [[keep.tile([P, PASSES, HALF, PACK], BF16, name="wg%d%d" % (h, e), align_bytes=64) for e in range(E)] for h in range(2)]
         t_codes = keep.tile([P, PASSES, E * C], U32, name="t_codes", align_bytes=64)
         t_scales = keep.tile([P, PASSES, E * C], U8, name="t_scales", align_bytes=64)
-        wa_codes = keep.tile([P, E, PASSES, HALF], U32, name="wa_codes", align_bytes=64)
-        wa_scales = keep.tile([P, E, PASSES, HALF], U8, name="wa_scales", align_bytes=64)
-        wb_codes = keep.tile([P, NB - 2, E, PASSES * P], U32, name="wb_codes", align_bytes=64)
-        wb_scales = keep.tile([P, NB - 2, E, PASSES * P], U8, name="wb_scales", align_bytes=64)
+        w_codes = keep.tile([P, 2, E, PASSES * HALF], U32, name="w_codes", align_bytes=64)
+        w_scales = keep.tile([P, 2, E, PASSES * HALF], U8, name="w_scales", align_bytes=64)
         y = [keep.tile([P, E * C], F32, name="y%d" % nb) for nb in range(NB)]
         banks = [[psum.tile([P, 2 * C], F32, name="ps%d%d" % (nb, pr)) for pr in range(E // 2)] for nb in range(NB)]
+
+        nc.sync.dma_start(offs_t[:], offs)
+        x_view = xT.rearrange("(g p t) n -> g p t n", p=P, t=PACK)
+        def load_x(g, t0, t1):
+            nc.sync.dma_start(xf[g][:, t0:t1, :], x_view[g, :, t0:t1, :])
+
+        load_x(0, 0, 1)
+        load_x(0, 1, 2)
+        load_x(1, 0, 2)
+        load_x(0, 2, 3)
+        load_x(0, 3, 4)
+        load_x(1, 2, 4)
+
+        def load_w(h, e):
+            for g in range(PASSES):
+                nc.sync.dma_start(
+                    wh[h][e][:, g, :, :],
+                    w[e, g * K_PASS : (g + 1) * K_PASS, h * HALF : (h + 1) * HALF].rearrange("(p j) n -> p j n", j=PACK),
+                )
+
+        def load_gate(h):
+            for r in range(2):
+                nc.sync.dma_start(gt[r][h][:], gate[r, h * HALF : (h + 1) * HALF, :].rearrange("(b p) t -> p b t", p=P))
+
+        for h in range(2):
+            for e in range(E):
+                load_w(h, e)
+        nc.sync.dma_start(pos_t[0][:], pos1)
+        nc.sync.dma_start(pos_t[1][:], pos2)
+        load_gate(0)
+        load_gate(1)
+
+        def slots(e):
+            return offs_t[:, e * LC : (e + 1) * LC]
+
+        def v_gather(e, t):
+            nc.vector.tensor_copy(tg[0][e][:, :, t], xf[0][:, t, :].indirect(slots(e)))
+
+        def s_gather(e, t):
+            nc.scalar.activation(tg[1][e][:, :, t], xb[:, t, :].indirect(slots(e)), COPY)
 
         tok_done = set()
         w_done = set()
@@ -96,114 +96,130 @@ def tile_routed_moe_kernel(tc, xT, w, gate, offs, pos1, pos2, out):
         def emit_matmuls():
             for nb in range(NB):
                 for e in range(E):
-                    if (nb, e) in mm_done:
+                    h = nb // 2
+                    if (nb, e) in mm_done or (h, e) not in w_done:
                         continue
-                    if not all((g, e) in tok_done and (nb, e, g) in w_done for g in range(PASSES)):
+                    if not all((g, e) in tok_done for g in range(PASSES)):
                         continue
                     if e % 2 == 1 and (nb, e - 1) not in mm_done:
                         continue
-                    bank = banks[nb][e // 2]
                     for g in range(PASSES):
-                        if nb < 2:
-                            lhs_codes = wa_codes[:, e, g, nb * P : (nb + 1) * P]
-                            lhs_scales = wa_scales[:, e, g, nb * P : (nb + 1) * P]
-                        else:
-                            lhs_codes = wb_codes[:, nb - 2, e, g * P : (g + 1) * P]
-                            lhs_scales = wb_scales[:, nb - 2, e, g * P : (g + 1) * P]
+                        c0 = g * HALF + (nb % 2) * P
                         nc.tensor.matmul_mx(
-                            out=bank[:, (e % 2) * C : (e % 2 + 1) * C],
-                            lhsT=lhs_codes.bitcast(FP8X4),
-                            lhsT_scale=lhs_scales,
+                            out=banks[nb][e // 2][:, (e % 2) * C : (e % 2 + 1) * C],
+                            lhsT=w_codes[:, h, e, c0 : c0 + P].bitcast(FP8X4),
+                            lhsT_scale=w_scales[:, h, e, c0 : c0 + P],
                             rhs=t_codes[:, g, e * C : (e + 1) * C].bitcast(FP8X4),
                             rhs_scale=t_scales[:, g, e * C : (e + 1) * C],
                             start=(g == 0),
                             stop=(g == PASSES - 1),
                         )
                     mm_done.add((nb, e))
-                    if e % 2 == 1:
-                        nc.scalar.copy(out=y[nb][:, (e - 1) * C : (e + 1) * C], in_=bank[:])
 
-        def token_gather(g, e):
-            g4 = gath.tile([P, PACK, C], F32, name="g4")
-            for t in range(PACK):
-                nc.vector.tensor_copy(g4[:, t, :], planes[g][t][:].indirect(offs_t[:, e * (C // 16) : (e + 1) * (C // 16)]))
-            grouped = tgrp.tile([P, C, PACK], BF16, name="tg", align_bytes=64)
-            interleave(nc.scalar.copy, grouped[:], g4[:])
-            return grouped
-
-        def token_quantize(g, e, grouped):
+        def t_quant(g, e):
             nc.vector.quantize_mx(
                 out=t_codes[:, g, e * C : (e + 1) * C].bitcast(FP8X4),
                 scales=t_scales[:, g, e * C : (e + 1) * C],
-                in_=grouped[:].rearrange("p c t -> p (c t)"),
+                in_=tg[g][e][:].rearrange("p c t -> p (c t)"),
             )
             tok_done.add((g, e))
-
-        def half_interleave(e, g):
-            grouped = wgh.tile([P, HALF, PACK], BF16, name="wg", align_bytes=64)
-            interleave(nc.scalar.copy, grouped[:], w_raw[e][g][:, :, 0:HALF])
-            return grouped
-
-        def half_quantize(e, g, grouped):
-            nc.vector.quantize_mx(
-                out=wa_codes[:, e, g, :].bitcast(FP8X4),
-                scales=wa_scales[:, e, g, :],
-                in_=grouped[:].rearrange("p c t -> p (c t)"),
-            )
-            w_done.add((0, e, g))
-            w_done.add((1, e, g))
-
-        def block_interleave(nb, e):
-            grouped = wgq.tile([P, PASSES, P, PACK], BF16, name="wg", align_bytes=64)
-            for g in range(PASSES):
-                interleave(nc.scalar.copy, grouped[:, g, :, :], w_raw[e][g][:, :, nb * P : (nb + 1) * P])
-            return grouped
-
-        def block_quantize(nb, e, grouped):
-            nc.vector.quantize_mx(
-                out=wb_codes[:, nb - 2, e, :].bitcast(FP8X4),
-                scales=wb_scales[:, nb - 2, e, :],
-                in_=grouped[:].rearrange("p g c t -> p (g c t)"),
-            )
-            for g in range(PASSES):
-                w_done.add((nb, e, g))
-
-        w_order = [(e, g) for e in range(E) for g in range(PASSES)]
-        pending = []
-        for i in range(len(TOKEN_ORDER)):
-            g, e = TOKEN_ORDER[i]
-            tg = token_gather(g, e)
-            we, wpass = w_order[i]
-            wgr = half_interleave(we, wpass)
-            for job in pending:
-                job()
             emit_matmuls()
-            pending = [
-                lambda g=g, e=e, tg=tg: token_quantize(g, e, tg),
-                lambda we=we, wpass=wpass, wgr=wgr: half_quantize(we, wpass, wgr),
-            ]
-        for job in pending:
-            job()
-        emit_matmuls()
 
-        jobs = []
-        ran = 0
-        for nb in range(2, NB):
-            for e in range(E):
-                wgr = block_interleave(nb, e)
-                jobs.append(lambda e=e, nb=nb, wgr=wgr: block_quantize(nb, e, wgr))
-                if len(jobs) - ran > 1:
-                    jobs[ran]()
-                    ran += 1
-                    emit_matmuls()
-        for job in jobs[ran:]:
-            job()
-        emit_matmuls()
+        def wi(copy_fn, h, e, g):
+            copy_fn(
+                out=wg[h][e][:, g, :, :].rearrange("p (c i) t -> p c t i", i=4),
+                in_=wh[h][e][:, g, :, :].rearrange("p t (c i) -> p c t i", i=4),
+            )
 
-        for nb in range(NB):
-            part = [comb.tile([P, T], F32, name="part%d" % r) for r in range(2)]
-            for r in range(2):
-                nc.vector.tensor_tensor(part[r][:], y[nb][:].indirect(pos_t[r][:]), gates[r][nb][:], MULT)
+        def wq(h, e):
+            nc.vector.quantize_mx(
+                out=w_codes[:, h, e, :].bitcast(FP8X4),
+                scales=w_scales[:, h, e, :],
+                in_=wg[h][e][:].rearrange("p g c t -> p (g c t)"),
+            )
+            w_done.add((h, e))
+            emit_matmuls()
+
+        def drain(nb, pr):
+            nc.scalar.copy(out=y[nb][:, pr * 2 * C : (pr + 1) * 2 * C], in_=banks[nb][pr][:])
+
+        parts = {}
+
+        def fetch(nb, r):
+            parts[(nb, r)] = comb.tile([P, T], F32, name="part%d" % r)
+            nc.vector.tensor_tensor(parts[(nb, r)][:], y[nb][:].indirect(pos_t[r][:]), gt[r][nb // 2][:, nb % 2, :], MULT)
+
+        def finish(nb):
             total = comb.tile([P, T], F32, name="total")
-            nc.vector.tensor_tensor(total[:], part[0][:], part[1][:], ADD)
+            nc.vector.tensor_tensor(total[:], parts[(nb, 0)][:], parts[(nb, 1)][:], ADD)
             nc.sync.dma_start(out[nb * P : (nb + 1) * P, :], total[:])
+
+        V = nc.vector.tensor_copy
+        S = nc.scalar.copy
+
+        nc.vector.memset(warm_in[:], 0.0)
+        nc.scalar.copy(out=warm_out[:], in_=warm_in[:])
+        for t0 in (0, 2):
+            nc.scalar.copy(out=xb[:, t0 : t0 + 2, :], in_=xf[1][:, t0 : t0 + 2, :])
+            for e in (0, 1):
+                for t in (t0, t0 + 1):
+                    s_gather(e, t)
+        for e in (2, 3):
+            for t in range(PACK):
+                s_gather(e, t)
+
+        for e in range(E):
+            for t in range(PACK):
+                v_gather(e, t)
+            if e > 0:
+                t_quant(0, e - 1)
+        wi(V, 0, 0, 0)
+        wi(V, 0, 0, 1)
+        t_quant(0, 3)
+        wi(V, 0, 1, 0)
+        wi(V, 0, 1, 1)
+        wq(0, 0)
+        t_quant(1, 0)
+        wi(V, 0, 2, 0)
+        wi(V, 0, 2, 1)
+        wq(0, 1)
+        t_quant(1, 1)
+        wi(S, 1, 0, 0)
+        wi(S, 1, 0, 1)
+        wi(S, 1, 1, 0)
+        wi(S, 1, 1, 1)
+        drain(0, 0)
+        drain(1, 0)
+        wi(V, 0, 3, 0)
+        wi(V, 0, 3, 1)
+        wq(0, 2)
+        t_quant(1, 2)
+        t_quant(1, 3)
+        wq(0, 3)
+        wi(S, 1, 2, 0)
+        wi(S, 1, 2, 1)
+        drain(0, 1)
+        drain(1, 1)
+        wq(1, 0)
+        wq(1, 1)
+        wi(V, 1, 3, 0)
+        wi(V, 1, 3, 1)
+        drain(2, 0)
+        drain(3, 0)
+
+        fetch(0, 0)
+        fetch(0, 1)
+        wq(1, 2)
+        finish(0)
+        fetch(1, 0)
+        wq(1, 3)
+        drain(2, 1)
+        drain(3, 1)
+        fetch(1, 1)
+        fetch(2, 0)
+        finish(1)
+        fetch(2, 1)
+        fetch(3, 0)
+        finish(2)
+        fetch(3, 1)
+        finish(3)

@@ -29,6 +29,7 @@ def tile_routed_moe_kernel(tc, xT, w, gate, offs, pos1, pos2, out):
     with ExitStack() as ctx:
         lists = ctx.enter_context(tc.tile_pool(name="lists", bufs=1))
         keep = ctx.enter_context(tc.tile_pool(name="keep", bufs=1))
+        ring = ctx.enter_context(tc.tile_pool(name="ring", bufs=4))
         comb = ctx.enter_context(tc.tile_pool(name="comb", bufs=3))
         psum = ctx.enter_context(tc.psum_pool(name="psum", bufs=1))
 
@@ -41,7 +42,7 @@ def tile_routed_moe_kernel(tc, xT, w, gate, offs, pos1, pos2, out):
         wh = [[keep.tile([P, PASSES, PACK, HALF], F32, name="wh%d%d" % (h, e)) for e in range(E)] for h in range(2)]
         gt = [[keep.tile([P, 2, T], F32, name="gt%d%d" % (r, h)) for h in range(2)] for r in range(2)]
         tg = [[keep.tile([P, C, PACK], BF16, name="tg%d%d" % (g, e), align_bytes=64) for e in range(E)] for g in range(PASSES)]
-        wg = [[keep.tile([P, PASSES, HALF, PACK], BF16, name="wg%d%d" % (h, e), align_bytes=64) for e in range(E)] for h in range(2)]
+        wg = [[ring.tile([P, PASSES, HALF, PACK], BF16, name="wg", align_bytes=64) for e in range(E)] for h in range(2)]
         t_codes = keep.tile([P, PASSES, E * C], U32, name="t_codes", align_bytes=64)
         t_scales = keep.tile([P, PASSES, E * C], U8, name="t_scales", align_bytes=64)
         w_codes = keep.tile([P, 2, E, PASSES * HALF], U32, name="w_codes", align_bytes=64)
@@ -89,32 +90,19 @@ def tile_routed_moe_kernel(tc, xT, w, gate, offs, pos1, pos2, out):
         def s_gather(e, t):
             nc.scalar.activation(tg[1][e][:, :, t], xb[:, t, :].indirect(slots(e)), COPY)
 
-        tok_done = set()
-        w_done = set()
-        mm_done = set()
-
-        def emit_matmuls():
-            for nb in range(NB):
-                for e in range(E):
-                    h = nb // 2
-                    if (nb, e) in mm_done or (h, e) not in w_done:
-                        continue
-                    if not all((g, e) in tok_done for g in range(PASSES)):
-                        continue
-                    if e % 2 == 1 and (nb, e - 1) not in mm_done:
-                        continue
-                    for g in range(PASSES):
-                        c0 = g * HALF + (nb % 2) * P
-                        nc.tensor.matmul_mx(
-                            out=banks[nb][e // 2][:, (e % 2) * C : (e % 2 + 1) * C],
-                            lhsT=w_codes[:, h, e, c0 : c0 + P].bitcast(FP8X4),
-                            lhsT_scale=w_scales[:, h, e, c0 : c0 + P],
-                            rhs=t_codes[:, g, e * C : (e + 1) * C].bitcast(FP8X4),
-                            rhs_scale=t_scales[:, g, e * C : (e + 1) * C],
-                            start=(g == 0),
-                            stop=(g == PASSES - 1),
-                        )
-                    mm_done.add((nb, e))
+        def mm(nb, e):
+            h = nb // 2
+            for g in range(PASSES):
+                c0 = g * HALF + (nb % 2) * P
+                nc.tensor.matmul_mx(
+                    out=banks[nb][e // 2][:, (e % 2) * C : (e % 2 + 1) * C],
+                    lhsT=w_codes[:, h, e, c0 : c0 + P].bitcast(FP8X4),
+                    lhsT_scale=w_scales[:, h, e, c0 : c0 + P],
+                    rhs=t_codes[:, g, e * C : (e + 1) * C].bitcast(FP8X4),
+                    rhs_scale=t_scales[:, g, e * C : (e + 1) * C],
+                    start=(g == 0),
+                    stop=(g == PASSES - 1),
+                )
 
         def t_quant(g, e):
             nc.vector.quantize_mx(
@@ -122,8 +110,6 @@ def tile_routed_moe_kernel(tc, xT, w, gate, offs, pos1, pos2, out):
                 scales=t_scales[:, g, e * C : (e + 1) * C],
                 in_=tg[g][e][:].rearrange("p c t -> p (c t)"),
             )
-            tok_done.add((g, e))
-            emit_matmuls()
 
         def wi(copy_fn, h, e, g):
             copy_fn(
@@ -137,8 +123,6 @@ def tile_routed_moe_kernel(tc, xT, w, gate, offs, pos1, pos2, out):
                 scales=w_scales[:, h, e, :],
                 in_=wg[h][e][:].rearrange("p g c t -> p (g c t)"),
             )
-            w_done.add((h, e))
-            emit_matmuls()
 
         def drain(nb, pr):
             nc.scalar.copy(out=y[nb][:, pr * 2 * C : (pr + 1) * 2 * C], in_=banks[nb][pr][:])
@@ -180,41 +164,52 @@ def tile_routed_moe_kernel(tc, xT, w, gate, offs, pos1, pos2, out):
         wi(V, 0, 1, 1)
         wq(0, 0)
         t_quant(1, 0)
+        mm(0, 0)
+        mm(1, 0)
         wi(V, 0, 2, 0)
         wi(V, 0, 2, 1)
         wq(0, 1)
         t_quant(1, 1)
+        mm(0, 1)
+        mm(1, 1)
         wi(S, 1, 0, 0)
-        wi(S, 1, 0, 1)
-        wi(S, 1, 1, 0)
-        wi(S, 1, 1, 1)
         drain(0, 0)
         drain(1, 0)
         wi(V, 0, 3, 0)
         wi(V, 0, 3, 1)
         wq(0, 2)
         t_quant(1, 2)
+        mm(0, 2)
+        mm(1, 2)
+        wi(V, 1, 2, 0)
         t_quant(1, 3)
         wq(0, 3)
-        wi(S, 1, 2, 0)
-        wi(S, 1, 2, 1)
+        mm(0, 3)
+        mm(1, 3)
+        wi(S, 1, 0, 1)
         drain(0, 1)
         drain(1, 1)
-        wq(1, 0)
-        wq(1, 1)
+        wi(S, 1, 1, 0)
+        wi(S, 1, 1, 1)
+        wi(V, 1, 2, 1)
         wi(V, 1, 3, 0)
         wi(V, 1, 3, 1)
-        drain(2, 0)
-        drain(3, 0)
 
         fetch(0, 0)
         fetch(0, 1)
         wq(1, 2)
-        finish(0)
-        fetch(1, 0)
         wq(1, 3)
-        drain(2, 1)
-        drain(3, 1)
+        finish(0)
+        wq(1, 0)
+        wq(1, 1)
+        for nb in (2, 3):
+            mm(nb, 2)
+            mm(nb, 3)
+            drain(nb, 1)
+            mm(nb, 0)
+            mm(nb, 1)
+            drain(nb, 0)
+        fetch(1, 0)
         fetch(1, 1)
         fetch(2, 0)
         finish(1)

@@ -21,6 +21,10 @@ K_PASS = P * PACK
 PASSES = K // K_PASS
 NB = N // P
 HALF = 2 * P
+LATE = {(1, 0): "wh00", (1, 1): "wh01", (1, 2): "wh02", (1, 3): "wh03"}
+W_LATE = {(1, 2): "wh10", (1, 3): "wh11"}
+Y_TAGS = ("y0", "y1", "y2", "y3")
+W_ORDER = ((1, 2), (1, 3), (0, 0), (0, 1), (0, 2), (0, 3), (1, 0), (1, 1))
 LC = C // 16
 
 
@@ -39,15 +43,36 @@ def tile_routed_moe_kernel(tc, xT, w, gate, offs, pos1, pos2, out):
         warm_out = keep.tile([P, 8], F32, name="warm_out")
         xf = [keep.tile([P, PACK, T], F32, name="xf%d" % g) for g in range(PASSES)]
         xb = keep.tile([P, PACK, T], BF16, name="xb")
-        wh = [[keep.tile([P, PASSES, PACK, HALF], F32, name="wh%d%d" % (h, e)) for e in range(E)] for h in range(2)]
+        wh = [[keep.tile([P, PASSES, PACK, HALF], F32, name="wh%d%d" % (h, e), align_bytes=64) for e in range(E)] for h in range(2)]
         gt = [[keep.tile([P, 2, T], F32, name="gt%d%d" % (r, h)) for h in range(2)] for r in range(2)]
         tg = [[keep.tile([P, C, PACK], BF16, name="tg%d%d" % (g, e), align_bytes=64) for e in range(E)] for g in range(PASSES)]
-        wg = [[ring.tile([P, PASSES, HALF, PACK], BF16, name="wg", align_bytes=64) for e in range(E)] for h in range(2)]
+        wg = [[None] * E, [None] * E]
+        for h, e in ((0, 0), (0, 1), (0, 2), (0, 3), (1, 0), (1, 1)):
+            wg[h][e] = ring.tile([P, PASSES, HALF, PACK], BF16, name="wg", align_bytes=64)
+        for e in (2, 3):
+            wg[1][e] = keep.tile([P, PASSES, HALF, PACK], BF16, name="wgs%d" % e, align_bytes=64)
         t_codes = keep.tile([P, PASSES, E * C], U32, name="t_codes", align_bytes=64)
         t_scales = keep.tile([P, PASSES, E * C], U8, name="t_scales", align_bytes=64)
+        late = {}
+        w_late = {}
+
+        def wcodes(h, e):
+            if (h, e) in W_LATE:
+                if (h, e) not in w_late:
+                    w_late[(h, e)] = keep.tile([P, PASSES * HALF], U32, name=W_LATE[(h, e)], align_bytes=64)
+                return w_late[(h, e)][:]
+            return w_codes[:, h, e, :]
+
+        def tok(g, e):
+            if (g, e) in LATE:
+                if (g, e) not in late:
+                    late[(g, e)] = keep.tile([P, C], U32, name=LATE[(g, e)], align_bytes=64)
+                return late[(g, e)][:], t_scales[:, g, e * C : (e + 1) * C]
+            return t_codes[:, g, e * C : (e + 1) * C], t_scales[:, g, e * C : (e + 1) * C]
+
         w_codes = keep.tile([P, 2, E, PASSES * HALF], U32, name="w_codes", align_bytes=64)
         w_scales = keep.tile([P, 2, E, PASSES * HALF], U8, name="w_scales", align_bytes=64)
-        y = [keep.tile([P, E * C], F32, name="y%d" % nb) for nb in range(NB)]
+        y = {}
         banks = [[psum.tile([P, 2 * C], F32, name="ps%d%d" % (nb, pr)) for pr in range(E // 2)] for nb in range(NB)]
 
         nc.sync.dma_start(offs_t[:], offs)
@@ -73,9 +98,8 @@ def tile_routed_moe_kernel(tc, xT, w, gate, offs, pos1, pos2, out):
             for r in range(2):
                 nc.sync.dma_start(gt[r][h][:], gate[r, h * HALF : (h + 1) * HALF, :].rearrange("(b p) t -> p b t", p=P))
 
-        for h in range(2):
-            for e in range(E):
-                load_w(h, e)
+        for h, e in W_ORDER:
+            load_w(h, e)
         nc.sync.dma_start(pos_t[0][:], pos1)
         nc.sync.dma_start(pos_t[1][:], pos2)
         load_gate(0)
@@ -96,18 +120,18 @@ def tile_routed_moe_kernel(tc, xT, w, gate, offs, pos1, pos2, out):
                 c0 = g * HALF + (nb % 2) * P
                 nc.tensor.matmul_mx(
                     out=banks[nb][e // 2][:, (e % 2) * C : (e % 2 + 1) * C],
-                    lhsT=w_codes[:, h, e, c0 : c0 + P].bitcast(FP8X4),
+                    lhsT=wcodes(h, e)[:, c0 : c0 + P].bitcast(FP8X4),
                     lhsT_scale=w_scales[:, h, e, c0 : c0 + P],
-                    rhs=t_codes[:, g, e * C : (e + 1) * C].bitcast(FP8X4),
-                    rhs_scale=t_scales[:, g, e * C : (e + 1) * C],
+                    rhs=tok(g, e)[0].bitcast(FP8X4),
+                    rhs_scale=tok(g, e)[1],
                     start=(g == 0),
                     stop=(g == PASSES - 1),
                 )
 
         def t_quant(g, e):
             nc.vector.quantize_mx(
-                out=t_codes[:, g, e * C : (e + 1) * C].bitcast(FP8X4),
-                scales=t_scales[:, g, e * C : (e + 1) * C],
+                out=tok(g, e)[0].bitcast(FP8X4),
+                scales=tok(g, e)[1],
                 in_=tg[g][e][:].rearrange("p c t -> p (c t)"),
             )
 
@@ -119,12 +143,14 @@ def tile_routed_moe_kernel(tc, xT, w, gate, offs, pos1, pos2, out):
 
         def wq(h, e):
             nc.vector.quantize_mx(
-                out=w_codes[:, h, e, :].bitcast(FP8X4),
+                out=wcodes(h, e).bitcast(FP8X4),
                 scales=w_scales[:, h, e, :],
                 in_=wg[h][e][:].rearrange("p g c t -> p (g c t)"),
             )
 
         def drain(nb, pr):
+            if nb not in y:
+                y[nb] = keep.tile([P, E * C], F32, name=Y_TAGS[nb], align_bytes=64)
             nc.scalar.copy(out=y[nb][:, pr * 2 * C : (pr + 1) * 2 * C], in_=banks[nb][pr][:])
 
         parts = {}
@@ -157,59 +183,37 @@ def tile_routed_moe_kernel(tc, xT, w, gate, offs, pos1, pos2, out):
                 v_gather(e, t)
             if e > 0:
                 t_quant(0, e - 1)
-        wi(V, 0, 0, 0)
-        wi(V, 0, 0, 1)
+        for e in (2, 3):
+            wi(S, 1, e, 0)
+            wi(S, 1, e, 1)
         t_quant(0, 3)
-        wi(V, 0, 1, 0)
-        wi(V, 0, 1, 1)
-        wq(0, 0)
-        t_quant(1, 0)
-        mm(0, 0)
-        mm(1, 0)
-        wi(V, 0, 2, 0)
-        wi(V, 0, 2, 1)
-        wq(0, 1)
-        t_quant(1, 1)
-        mm(0, 1)
-        mm(1, 1)
-        wi(S, 1, 0, 0)
-        drain(0, 0)
-        drain(1, 0)
-        wi(V, 0, 3, 0)
-        wi(V, 0, 3, 1)
-        wq(0, 2)
-        t_quant(1, 2)
-        mm(0, 2)
-        mm(1, 2)
-        wi(V, 1, 2, 0)
-        t_quant(1, 3)
-        wq(0, 3)
-        mm(0, 3)
-        mm(1, 3)
-        wi(S, 1, 0, 1)
-        drain(0, 1)
-        drain(1, 1)
-        wi(S, 1, 1, 0)
-        wi(S, 1, 1, 1)
-        wi(V, 1, 2, 1)
-        wi(V, 1, 3, 0)
-        wi(V, 1, 3, 1)
-
-        fetch(0, 0)
-        fetch(0, 1)
-        wq(1, 2)
-        wq(1, 3)
-        finish(0)
-        wq(1, 0)
-        wq(1, 1)
+        for e in range(E):
+            wi(V, 0, e, 0)
+            wi(V, 0, e, 1)
+            wq(0, e)
+            t_quant(1, e)
+            mm(0, e)
+            mm(1, e)
+            if e % 2 == 1:
+                drain(0, e // 2)
+                drain(1, e // 2)
+        for e in range(2):
+            wi(V, 1, e, 0)
+            wi(V, 1, e, 1)
+            wq(1, e)
+            wq(1, e + 2)
         for nb in (2, 3):
-            mm(nb, 2)
-            mm(nb, 3)
-            drain(nb, 1)
             mm(nb, 0)
             mm(nb, 1)
             drain(nb, 0)
+            mm(nb, 2)
+            mm(nb, 3)
+            drain(nb, 1)
+
+        fetch(0, 0)
+        fetch(0, 1)
         fetch(1, 0)
+        finish(0)
         fetch(1, 1)
         fetch(2, 0)
         finish(1)

@@ -11,21 +11,19 @@ U32 = mybir.dt.uint32
 U16 = mybir.dt.uint16
 U8 = mybir.dt.uint8
 FP8X4 = mybir.dt.float8_e4m3fn_x4
-MULT = mybir.AluOpType.mult
-ADD = mybir.AluOpType.add
-COPY = mybir.ActivationFunctionType.Copy
 
 P = 128
 PACK = 4
 K_PASS = P * PACK
 PASSES = K // K_PASS
-NB = N // P
-HALF = 2 * P
-LATE = {(1, 0): "wh00", (1, 1): "wh01", (1, 2): "wh02", (1, 3): "wh03"}
-W_LATE = {(1, 2): "wh10", (1, 3): "wh11"}
-Y_TAGS = ("y0", "y1", "y2", "y3")
-W_ORDER = ((1, 2), (1, 3), (0, 0), (0, 1), (0, 2), (0, 3), (1, 0), (1, 1))
-LC = C // 16
+BLOCKS = N // P
+HALF = N // 2
+LIST_COLS = C // 16
+MX_ALIGN = 64
+
+LAST = E - 1
+SCALAR_EXPERTS = (0, 1)
+WHOLE_EXPERT = 2
 
 
 def tile_routed_moe_kernel(tc, xT, w, gate, offs, pos1, pos2, out):
@@ -33,192 +31,225 @@ def tile_routed_moe_kernel(tc, xT, w, gate, offs, pos1, pos2, out):
     with ExitStack() as ctx:
         lists = ctx.enter_context(tc.tile_pool(name="lists", bufs=1))
         keep = ctx.enter_context(tc.tile_pool(name="keep", bufs=1))
-        ring = ctx.enter_context(tc.tile_pool(name="ring", bufs=4))
-        comb = ctx.enter_context(tc.tile_pool(name="comb", bufs=3))
+        back = ctx.enter_context(tc.tile_pool(name="back", bufs=3))
         psum = ctx.enter_context(tc.psum_pool(name="psum", bufs=1))
 
-        offs_t = lists.tile([P, E * C // 16], U16, name="offs_t")
-        pos_t = [lists.tile([P, T // 16], U16, name="pos_t%d" % r) for r in range(2)]
-        warm_in = keep.tile([P, 8], F32, name="warm_in")
-        warm_out = keep.tile([P, 8], F32, name="warm_out")
-        xf = [keep.tile([P, PACK, T], F32, name="xf%d" % g) for g in range(PASSES)]
-        xb = keep.tile([P, PACK, T], BF16, name="xb")
-        wh = [[keep.tile([P, PASSES, PACK, HALF], F32, name="wh%d%d" % (h, e), align_bytes=64) for e in range(E)] for h in range(2)]
-        gt = [[keep.tile([P, 2, T], F32, name="gt%d%d" % (r, h)) for h in range(2)] for r in range(2)]
-        tg = [[keep.tile([P, C, PACK], BF16, name="tg%d%d" % (g, e), align_bytes=64) for e in range(E)] for g in range(PASSES)]
-        wg = [[None] * E, [None] * E]
-        for h, e in ((0, 0), (0, 1), (0, 2), (0, 3), (1, 0), (1, 1)):
-            wg[h][e] = ring.tile([P, PASSES, HALF, PACK], BF16, name="wg", align_bytes=64)
-        for e in (2, 3):
-            wg[1][e] = keep.tile([P, PASSES, HALF, PACK], BF16, name="wgs%d" % e, align_bytes=64)
-        t_codes = keep.tile([P, PASSES, E * C], U32, name="t_codes", align_bytes=64)
-        t_scales = keep.tile([P, PASSES, E * C], U8, name="t_scales", align_bytes=64)
-        late = {}
-        w_late = {}
+        slot_token = lists.tile([P, E * C // 16], U16, name="slot_token")
+        token_slot = [lists.tile([P, T // 16], U16, name="token_slot%d" % r) for r in range(2)]
 
-        def wcodes(h, e):
-            if (h, e) in W_LATE:
-                if (h, e) not in w_late:
-                    w_late[(h, e)] = keep.tile([P, PASSES * HALF], U32, name=W_LATE[(h, e)], align_bytes=64)
-                return w_late[(h, e)][:]
-            return w_codes[:, h, e, :]
+        zeros = keep.tile([P, 8], F32, name="zeros")
+        zeros_copy = keep.tile([P, 8], F32, name="zeros_copy")
 
-        def tok(g, e):
-            if (g, e) in LATE:
-                if (g, e) not in late:
-                    late[(g, e)] = keep.tile([P, C], U32, name=LATE[(g, e)], align_bytes=64)
-                return late[(g, e)][:], t_scales[:, g, e * C : (e + 1) * C]
-            return t_codes[:, g, e * C : (e + 1) * C], t_scales[:, g, e * C : (e + 1) * C]
+        x_f32 = [keep.tile([P, PACK, T], F32, name="x_f32_%d" % g) for g in range(PASSES)]
+        x_bf16 = keep.tile([P, PACK, T], BF16, name="x_bf16")
 
-        w_codes = keep.tile([P, 2, E, PASSES * HALF], U32, name="w_codes", align_bytes=64)
-        w_scales = keep.tile([P, 2, E, PASSES * HALF], U8, name="w_scales", align_bytes=64)
-        y = {}
-        banks = [[psum.tile([P, 2 * C], F32, name="ps%d%d" % (nb, pr)) for pr in range(E // 2)] for nb in range(NB)]
+        w_f32 = {}
+        for e in range(LAST):
+            for g in range(PASSES):
+                w_f32[(e, g)] = keep.tile([P, PACK, N], F32, name="w_f32_%d%d" % (e, g), align_bytes=MX_ALIGN)
+        for h in range(2):
+            for g in range(PASSES):
+                w_f32[(LAST, g, h)] = keep.tile(
+                    [P, PACK, HALF], F32, name="w_f32_%d%d%d" % (LAST, g, h), align_bytes=MX_ALIGN
+                )
+        gate_sb = [[keep.tile([P, 2, T], F32, name="gate_sb%d%d" % (r, h)) for h in range(2)] for r in range(2)]
 
-        nc.sync.dma_start(offs_t[:], offs)
-        x_view = xT.rearrange("(g p t) n -> g p t n", p=P, t=PACK)
-        def load_x(g, t0, t1):
-            nc.sync.dma_start(xf[g][:, t0:t1, :], x_view[g, :, t0:t1, :])
+        tokens_bf16 = [
+            [keep.tile([P, C, PACK], BF16, name="tokens_bf16_%d%d" % (g, e), align_bytes=MX_ALIGN) for e in range(E)]
+            for g in range(PASSES)
+        ]
+        weights_bf16 = [
+            [
+                keep.tile([P, PASSES, HALF, PACK], BF16, name="weights_bf16_%d%d" % (h, e), align_bytes=MX_ALIGN)
+                for e in range(E)
+            ]
+            for h in range(2)
+        ]
 
-        load_x(0, 0, 1)
-        load_x(0, 1, 2)
-        load_x(1, 0, 2)
-        load_x(0, 2, 3)
-        load_x(0, 3, 4)
-        load_x(1, 2, 4)
+        token_codes_0 = keep.tile([P, E * C], U32, name="token_codes_0", align_bytes=MX_ALIGN)
+        token_codes_1 = {}
+        token_scales = keep.tile([P, PASSES, E * C], U8, name="token_scales", align_bytes=MX_ALIGN)
+        weight_codes = {}
+        for h in range(2):
+            for e in range(E):
+                if not (h == 1 and e in SCALAR_EXPERTS):
+                    weight_codes[(h, e)] = keep.tile(
+                        [P, PASSES * HALF], U32, name="weight_codes_%d%d" % (h, e), align_bytes=MX_ALIGN
+                    )
+        weight_scales = keep.tile([P, 2, E, PASSES * HALF], U8, name="weight_scales", align_bytes=MX_ALIGN)
 
-        def load_w(h, e):
+        sums_psum = [
+            [psum.tile([P, 2 * C], F32, name="sums_psum%d%d" % (b, pair)) for pair in range(E // 2)]
+            for b in range(BLOCKS)
+        ]
+        sums_sb = [keep.tile([P, E * C], F32, name="sums_sb%d" % b) for b in range(BLOCKS)]
+
+        def heir(former_name, shape, dtype):
+            return keep.tile(shape, dtype, name=former_name, align_bytes=MX_ALIGN)
+
+        nc.sync.dma_start(slot_token[:], offs)
+        planes = xT.rearrange("(g p t) n -> g p t n", p=P, t=PACK)
+
+        def load_planes(g, t0, t1):
+            nc.sync.dma_start(x_f32[g][:, t0:t1, :], planes[g, :, t0:t1, :])
+
+        load_planes(0, 0, 1)
+        load_planes(0, 1, 2)
+        load_planes(1, 0, 2)
+        load_planes(0, 2, 3)
+        load_planes(0, 3, 4)
+        load_planes(1, 2, 4)
+        for e in range(LAST):
             for g in range(PASSES):
                 nc.sync.dma_start(
-                    wh[h][e][:, g, :, :],
-                    w[e, g * K_PASS : (g + 1) * K_PASS, h * HALF : (h + 1) * HALF].rearrange("(p j) n -> p j n", j=PACK),
+                    w_f32[(e, g)][:], w[e, g * K_PASS : (g + 1) * K_PASS, :].rearrange("(p j) n -> p j n", j=PACK)
+                )
+        for h in range(2):
+            for g in range(PASSES):
+                nc.sync.dma_start(
+                    w_f32[(LAST, g, h)][:],
+                    w[LAST, g * K_PASS : (g + 1) * K_PASS, h * HALF : (h + 1) * HALF].rearrange(
+                        "(p j) n -> p j n", j=PACK
+                    ),
+                )
+        nc.sync.dma_start(token_slot[0][:], pos1)
+        nc.sync.dma_start(token_slot[1][:], pos2)
+        for h in range(2):
+            for r in range(2):
+                nc.sync.dma_start(
+                    gate_sb[r][h][:], gate[r, h * HALF : (h + 1) * HALF, :].rearrange("(b p) t -> p b t", p=P)
                 )
 
-        def load_gate(h):
-            for r in range(2):
-                nc.sync.dma_start(gt[r][h][:], gate[r, h * HALF : (h + 1) * HALF, :].rearrange("(b p) t -> p b t", p=P))
+        def slots_of(e):
+            return slot_token[:, e * LIST_COLS : (e + 1) * LIST_COLS]
 
-        for h, e in W_ORDER:
-            load_w(h, e)
-        nc.sync.dma_start(pos_t[0][:], pos1)
-        nc.sync.dma_start(pos_t[1][:], pos2)
-        load_gate(0)
-        load_gate(1)
+        def gather_on_vector(e, t):
+            nc.vector.tensor_copy(tokens_bf16[0][e][:, :, t], x_f32[0][:, t, :].indirect(slots_of(e)))
 
-        def slots(e):
-            return offs_t[:, e * LC : (e + 1) * LC]
+        def gather_on_scalar(e, t):
+            nc.scalar.activation(
+                tokens_bf16[1][e][:, :, t], x_bf16[:, t, :].indirect(slots_of(e)), mybir.ActivationFunctionType.Copy
+            )
 
-        def v_gather(e, t):
-            nc.vector.tensor_copy(tg[0][e][:, :, t], xf[0][:, t, :].indirect(slots(e)))
+        def codes_of_tokens(g, e):
+            if g == 0:
+                return token_codes_0[:, e * C : (e + 1) * C]
+            return token_codes_1[e][:]
 
-        def s_gather(e, t):
-            nc.scalar.activation(tg[1][e][:, :, t], xb[:, t, :].indirect(slots(e)), COPY)
+        def quantize_tokens(g, e):
+            if g == 1:
+                token_codes_1[e] = heir("weights_bf16_0%d" % e, [P, C], U32)
+            nc.vector.quantize_mx(
+                out=codes_of_tokens(g, e).bitcast(FP8X4),
+                scales=token_scales[:, g, e * C : (e + 1) * C],
+                in_=tokens_bf16[g][e][:].rearrange("p c t -> p (c t)"),
+            )
 
-        def mm(nb, e):
-            h = nb // 2
+        def interleave_weights(copy, h, e, g):
+            if e == LAST:
+                rows = w_f32[(e, g, h)][:]
+            else:
+                rows = w_f32[(e, g)][:, :, h * HALF : (h + 1) * HALF]
+            copy(
+                out=weights_bf16[h][e][:, g, :, :].rearrange("p (c i) t -> p c t i", i=4),
+                in_=rows.rearrange("p t (c i) -> p c t i", i=4),
+            )
+
+        def quantize_weights(h, e):
+            nc.vector.quantize_mx(
+                out=weight_codes[(h, e)][:].bitcast(FP8X4),
+                scales=weight_scales[:, h, e, :],
+                in_=weights_bf16[h][e][:].rearrange("p g c t -> p (g c t)"),
+            )
+
+        def multiply(b, e):
+            h = b // 2
             for g in range(PASSES):
-                c0 = g * HALF + (nb % 2) * P
+                first = g * HALF + (b % 2) * P
                 nc.tensor.matmul_mx(
-                    out=banks[nb][e // 2][:, (e % 2) * C : (e % 2 + 1) * C],
-                    lhsT=wcodes(h, e)[:, c0 : c0 + P].bitcast(FP8X4),
-                    lhsT_scale=w_scales[:, h, e, c0 : c0 + P],
-                    rhs=tok(g, e)[0].bitcast(FP8X4),
-                    rhs_scale=tok(g, e)[1],
+                    out=sums_psum[b][e // 2][:, (e % 2) * C : (e % 2 + 1) * C],
+                    lhsT=weight_codes[(h, e)][:, first : first + P].bitcast(FP8X4),
+                    lhsT_scale=weight_scales[:, h, e, first : first + P],
+                    rhs=codes_of_tokens(g, e).bitcast(FP8X4),
+                    rhs_scale=token_scales[:, g, e * C : (e + 1) * C],
                     start=(g == 0),
                     stop=(g == PASSES - 1),
                 )
 
-        def t_quant(g, e):
-            nc.vector.quantize_mx(
-                out=tok(g, e)[0].bitcast(FP8X4),
-                scales=tok(g, e)[1],
-                in_=tg[g][e][:].rearrange("p c t -> p (c t)"),
+        def drain(b, pair):
+            nc.scalar.copy(out=sums_sb[b][:, pair * 2 * C : (pair + 1) * 2 * C], in_=sums_psum[b][pair][:])
+
+        fetched = {}
+
+        def fetch(b, r):
+            fetched[(b, r)] = back.tile([P, T], F32, name="fetched%d" % r)
+            nc.vector.tensor_tensor(
+                fetched[(b, r)][:],
+                sums_sb[b][:].indirect(token_slot[r][:]),
+                gate_sb[r][b // 2][:, b % 2, :],
+                mybir.AluOpType.mult,
             )
 
-        def wi(copy_fn, h, e, g):
-            copy_fn(
-                out=wg[h][e][:, g, :, :].rearrange("p (c i) t -> p c t i", i=4),
-                in_=wh[h][e][:, g, :, :].rearrange("p t (c i) -> p c t i", i=4),
-            )
+        def finish(b):
+            total = back.tile([P, T], F32, name="total")
+            nc.vector.tensor_tensor(total[:], fetched[(b, 0)][:], fetched[(b, 1)][:], mybir.AluOpType.add)
+            nc.sync.dma_start(out[b * P : (b + 1) * P, :], total[:])
 
-        def wq(h, e):
-            nc.vector.quantize_mx(
-                out=wcodes(h, e).bitcast(FP8X4),
-                scales=w_scales[:, h, e, :],
-                in_=wg[h][e][:].rearrange("p g c t -> p (g c t)"),
-            )
+        nc.vector.memset(zeros[:], 0.0)
+        nc.scalar.copy(out=zeros_copy[:], in_=zeros[:])
 
-        def drain(nb, pr):
-            if nb not in y:
-                y[nb] = keep.tile([P, E * C], F32, name=Y_TAGS[nb], align_bytes=64)
-            nc.scalar.copy(out=y[nb][:, pr * 2 * C : (pr + 1) * 2 * C], in_=banks[nb][pr][:])
-
-        parts = {}
-
-        def fetch(nb, r):
-            parts[(nb, r)] = comb.tile([P, T], F32, name="part%d" % r)
-            nc.vector.tensor_tensor(parts[(nb, r)][:], y[nb][:].indirect(pos_t[r][:]), gt[r][nb // 2][:, nb % 2, :], MULT)
-
-        def finish(nb):
-            total = comb.tile([P, T], F32, name="total")
-            nc.vector.tensor_tensor(total[:], parts[(nb, 0)][:], parts[(nb, 1)][:], ADD)
-            nc.sync.dma_start(out[nb * P : (nb + 1) * P, :], total[:])
-
-        V = nc.vector.tensor_copy
-        S = nc.scalar.copy
-
-        nc.vector.memset(warm_in[:], 0.0)
-        nc.scalar.copy(out=warm_out[:], in_=warm_in[:])
         for t0 in (0, 2):
-            nc.scalar.copy(out=xb[:, t0 : t0 + 2, :], in_=xf[1][:, t0 : t0 + 2, :])
+            nc.scalar.copy(out=x_bf16[:, t0 : t0 + 2, :], in_=x_f32[1][:, t0 : t0 + 2, :])
             for e in (0, 1):
                 for t in (t0, t0 + 1):
-                    s_gather(e, t)
+                    gather_on_scalar(e, t)
         for e in (2, 3):
             for t in range(PACK):
-                s_gather(e, t)
+                gather_on_scalar(e, t)
 
         for e in range(E):
             for t in range(PACK):
-                v_gather(e, t)
+                gather_on_vector(e, t)
             if e > 0:
-                t_quant(0, e - 1)
-        for e in (2, 3):
-            wi(S, 1, e, 0)
-            wi(S, 1, e, 1)
-        t_quant(0, 3)
+                quantize_tokens(0, e - 1)
+
+        for e in SCALAR_EXPERTS:
+            for g in range(PASSES):
+                interleave_weights(nc.scalar.copy, 1, e, g)
+        quantize_tokens(0, E - 1)
+
         for e in range(E):
-            wi(V, 0, e, 0)
-            wi(V, 0, e, 1)
-            wq(0, e)
-            t_quant(1, e)
-            mm(0, e)
-            mm(1, e)
+            halves = (0, 1) if e == WHOLE_EXPERT else (0,)
+            for g in range(PASSES):
+                for h in halves:
+                    interleave_weights(nc.vector.tensor_copy, h, e, g)
+            quantize_weights(0, e)
+            quantize_tokens(1, e)
+            multiply(0, e)
+            multiply(1, e)
             if e % 2 == 1:
                 drain(0, e // 2)
                 drain(1, e // 2)
-        for e in range(2):
-            wi(V, 1, e, 0)
-            wi(V, 1, e, 1)
-            wq(1, e)
-            wq(1, e + 2)
-        for nb in (2, 3):
-            mm(nb, 0)
-            mm(nb, 1)
-            drain(nb, 0)
-            mm(nb, 2)
-            mm(nb, 3)
-            drain(nb, 1)
+            if 1 in halves:
+                quantize_weights(1, e)
+
+        weight_codes[(1, 0)] = heir("w_f32_%d%d%d" % (LAST, 1, 0), [P, PASSES * HALF], U32)
+        quantize_weights(1, 0)
+        for g in range(PASSES):
+            interleave_weights(nc.vector.tensor_copy, 1, LAST, g)
+        weight_codes[(1, 1)] = heir("w_f32_%d%d%d" % (LAST, 1, 1), [P, PASSES * HALF], U32)
+        quantize_weights(1, 1)
+        quantize_weights(1, LAST)
+        for b in (2, 3):
+            for e in range(E):
+                multiply(b, e)
+                if e % 2 == 1:
+                    drain(b, e // 2)
 
         fetch(0, 0)
         fetch(0, 1)
-        fetch(1, 0)
-        finish(0)
-        fetch(1, 1)
-        fetch(2, 0)
-        finish(1)
-        fetch(2, 1)
-        fetch(3, 0)
-        finish(2)
-        fetch(3, 1)
-        finish(3)
+        for b in range(1, BLOCKS):
+            fetch(b, 0)
+            finish(b - 1)
+            fetch(b, 1)
+        finish(BLOCKS - 1)

@@ -20,10 +20,7 @@ BLOCKS = N // P
 HALF = N // 2
 LIST_COLS = C // 16
 MX_ALIGN = 64
-
 LAST = E - 1
-SCALAR_EXPERTS = (0, 1)
-WHOLE_EXPERT = 2
 
 
 def tile_routed_moe_kernel(tc, xT, w, gate, offs, pos1, pos2, out):
@@ -41,7 +38,8 @@ def tile_routed_moe_kernel(tc, xT, w, gate, offs, pos1, pos2, out):
         zeros_copy = keep.tile([P, 8], F32, name="zeros_copy")
 
         x_f32 = [keep.tile([P, PACK, T], F32, name="x_f32_%d" % g) for g in range(PASSES)]
-        x_bf16 = keep.tile([P, PACK, T], BF16, name="x_bf16")
+        x_bf16_1 = keep.tile([P, PACK, T], BF16, name="x_bf16_1")
+        x_bf16_0 = keep.tile([P, 2, T], BF16, name="x_bf16_0")
 
         w_f32 = {}
         for e in range(LAST):
@@ -66,16 +64,14 @@ def tile_routed_moe_kernel(tc, xT, w, gate, offs, pos1, pos2, out):
             for h in range(2)
         ]
 
-        token_codes_0 = keep.tile([P, E * C], U32, name="token_codes_0", align_bytes=MX_ALIGN)
-        token_codes_1 = {}
+        token_codes = {}
         token_scales = keep.tile([P, PASSES, E * C], U8, name="token_scales", align_bytes=MX_ALIGN)
         weight_codes = {}
         for h in range(2):
             for e in range(E):
-                if not (h == 1 and e in SCALAR_EXPERTS):
-                    weight_codes[(h, e)] = keep.tile(
-                        [P, PASSES * HALF], U32, name="weight_codes_%d%d" % (h, e), align_bytes=MX_ALIGN
-                    )
+                weight_codes[(h, e)] = keep.tile(
+                    [P, PASSES * HALF], U32, name="weight_codes_%d%d" % (h, e), align_bytes=MX_ALIGN
+                )
         weight_scales = keep.tile([P, 2, E, PASSES * HALF], U8, name="weight_scales", align_bytes=MX_ALIGN)
 
         sums_psum = [
@@ -93,12 +89,11 @@ def tile_routed_moe_kernel(tc, xT, w, gate, offs, pos1, pos2, out):
         def load_planes(g, t0, t1):
             nc.sync.dma_start(x_f32[g][:, t0:t1, :], planes[g, :, t0:t1, :])
 
+        load_planes(1, 0, 2)
         load_planes(0, 0, 1)
         load_planes(0, 1, 2)
-        load_planes(1, 0, 2)
-        load_planes(0, 2, 3)
-        load_planes(0, 3, 4)
         load_planes(1, 2, 4)
+        load_planes(0, 2, 4)
         for e in range(LAST):
             for g in range(PASSES):
                 nc.sync.dma_start(
@@ -126,21 +121,15 @@ def tile_routed_moe_kernel(tc, xT, w, gate, offs, pos1, pos2, out):
         def gather_on_vector(e, t):
             nc.vector.tensor_copy(tokens_bf16[0][e][:, :, t], x_f32[0][:, t, :].indirect(slots_of(e)))
 
-        def gather_on_scalar(e, t):
+        def gather_on_scalar(g, e, t):
+            window = x_bf16_1[:, t, :] if g == 1 else x_bf16_0[:, t - 2, :]
             nc.scalar.activation(
-                tokens_bf16[1][e][:, :, t], x_bf16[:, t, :].indirect(slots_of(e)), mybir.ActivationFunctionType.Copy
+                tokens_bf16[g][e][:, :, t], window.indirect(slots_of(e)), mybir.ActivationFunctionType.Copy
             )
 
-        def codes_of_tokens(g, e):
-            if g == 0:
-                return token_codes_0[:, e * C : (e + 1) * C]
-            return token_codes_1[e][:]
-
         def quantize_tokens(g, e):
-            if g == 1:
-                token_codes_1[e] = heir("weights_bf16_0%d" % e, [P, C], U32)
             nc.vector.quantize_mx(
-                out=codes_of_tokens(g, e).bitcast(FP8X4),
+                out=token_codes[e][:, g, :].bitcast(FP8X4),
                 scales=token_scales[:, g, e * C : (e + 1) * C],
                 in_=tokens_bf16[g][e][:].rearrange("p c t -> p (c t)"),
             )
@@ -170,7 +159,7 @@ def tile_routed_moe_kernel(tc, xT, w, gate, offs, pos1, pos2, out):
                     out=sums_psum[b][e // 2][:, (e % 2) * C : (e % 2 + 1) * C],
                     lhsT=weight_codes[(h, e)][:, first : first + P].bitcast(FP8X4),
                     lhsT_scale=weight_scales[:, h, e, first : first + P],
-                    rhs=codes_of_tokens(g, e).bitcast(FP8X4),
+                    rhs=token_codes[e][:, g, :].bitcast(FP8X4),
                     rhs_scale=token_scales[:, g, e * C : (e + 1) * C],
                     start=(g == 0),
                     stop=(g == PASSES - 1),
@@ -198,53 +187,58 @@ def tile_routed_moe_kernel(tc, xT, w, gate, offs, pos1, pos2, out):
         nc.vector.memset(zeros[:], 0.0)
         nc.scalar.copy(out=zeros_copy[:], in_=zeros[:])
 
-        for t0 in (0, 2):
-            nc.scalar.copy(out=x_bf16[:, t0 : t0 + 2, :], in_=x_f32[1][:, t0 : t0 + 2, :])
-            for e in (0, 1):
-                for t in (t0, t0 + 1):
-                    gather_on_scalar(e, t)
-        for e in (2, 3):
-            for t in range(PACK):
-                gather_on_scalar(e, t)
+        nc.scalar.copy(out=x_bf16_1[:, 0:2, :], in_=x_f32[1][:, 0:2, :])
+        for e in range(E):
+            gather_on_vector(e, 0)
+        nc.vector.tensor_copy(out=x_bf16_1[:, 2:4, :], in_=x_f32[1][:, 2:4, :])
+        for e in range(E):
+            gather_on_vector(e, 1)
+        nc.vector.tensor_copy(out=x_bf16_0[:], in_=x_f32[0][:, 2:4, :])
 
         for e in range(E):
-            for t in range(PACK):
-                gather_on_vector(e, t)
-            if e > 0:
-                quantize_tokens(0, e - 1)
-
-        for e in SCALAR_EXPERTS:
-            for g in range(PASSES):
-                interleave_weights(nc.scalar.copy, 1, e, g)
-        quantize_tokens(0, E - 1)
-
+            for t in (0, 1):
+                gather_on_scalar(1, e, t)
         for e in range(E):
-            halves = (0, 1) if e == WHOLE_EXPERT else (0,)
-            for g in range(PASSES):
-                for h in halves:
-                    interleave_weights(nc.vector.tensor_copy, h, e, g)
-            quantize_weights(0, e)
+            for t in (2, 3):
+                gather_on_scalar(1, e, t)
+            for t in (2, 3):
+                gather_on_scalar(0, e, t)
+
+        def tokens_and_products(e, former_name, blocks):
+            token_codes[e] = heir(former_name, [P, PASSES, C], U32)
             quantize_tokens(1, e)
-            multiply(0, e)
-            multiply(1, e)
-            if e % 2 == 1:
-                drain(0, e // 2)
-                drain(1, e // 2)
-            if 1 in halves:
-                quantize_weights(1, e)
+            quantize_tokens(0, e)
+            for b in blocks:
+                multiply(b, e)
 
-        weight_codes[(1, 0)] = heir("w_f32_%d%d%d" % (LAST, 1, 0), [P, PASSES * HALF], U32)
-        quantize_weights(1, 0)
+        for e in range(LAST):
+            for g in range(PASSES):
+                for h in range(2):
+                    interleave_weights(nc.vector.tensor_copy, h, e, g)
+            if e > 0:
+                tokens_and_products(e - 1, "w_f32_%d%d" % (e, 1), range(BLOCKS))
+            quantize_weights(0, e)
+            quantize_weights(1, e)
+        for g in range(PASSES):
+            interleave_weights(nc.vector.tensor_copy, 0, LAST, g)
+        tokens_and_products(LAST - 1, "w_f32_%d%d%d" % (LAST, 1, 0), (0, 1))
+        quantize_weights(0, LAST)
+        tokens_and_products(LAST, "weights_bf16_0%d" % LAST, (0, 1))
+        for b in (0, 1):
+            drain(b, 0)
+        for b in (0, 1):
+            drain(b, 1)
         for g in range(PASSES):
             interleave_weights(nc.vector.tensor_copy, 1, LAST, g)
-        weight_codes[(1, 1)] = heir("w_f32_%d%d%d" % (LAST, 1, 1), [P, PASSES * HALF], U32)
-        quantize_weights(1, 1)
+        for b in (2, 3):
+            multiply(b, LAST - 1)
         quantize_weights(1, LAST)
         for b in (2, 3):
-            for e in range(E):
-                multiply(b, e)
-                if e % 2 == 1:
-                    drain(b, e // 2)
+            multiply(b, LAST)
+        for b in (2, 3):
+            drain(b, 0)
+        for b in (2, 3):
+            drain(b, 1)
 
         fetch(0, 0)
         fetch(0, 1)

@@ -1,6 +1,7 @@
 from contextlib import ExitStack
 
 import concourse.mybir as mybir
+from concourse.masks import make_identity
 
 K, T, E, C, N = 1024, 512, 4, 256, 512
 FLOPS = 2 * K * N * E * C
@@ -21,6 +22,8 @@ HALF = N // 2
 LIST_COLS = C // 16
 MX_ALIGN = 64
 LAST = E - 1
+TENSOR_SUMS = 3
+assert TENSOR_SUMS * 2 * 2 * P * P * T <= FLOPS // 10
 
 
 def tile_routed_moe_kernel(tc, xT, w, gate, offs, pos1, pos2, out):
@@ -36,6 +39,7 @@ def tile_routed_moe_kernel(tc, xT, w, gate, offs, pos1, pos2, out):
 
         zeros = keep.tile([P, 8], F32, name="zeros")
         zeros_copy = keep.tile([P, 8], F32, name="zeros_copy")
+        identity = keep.tile([P, P], F32, name="identity")
 
         x_f32 = [keep.tile([P, PACK, T], F32, name="x_f32_%d" % g) for g in range(PASSES)]
         x_bf16_1 = keep.tile([P, PACK, T], BF16, name="x_bf16_1")
@@ -59,7 +63,7 @@ def tile_routed_moe_kernel(tc, xT, w, gate, offs, pos1, pos2, out):
         weights_bf16 = [
             [
                 keep.tile([P, PASSES, HALF, PACK], BF16, name="weights_bf16_%d%d" % (h, e), align_bytes=MX_ALIGN)
-                for e in range(E)
+                for e in range(E - h)
             ]
             for h in range(2)
         ]
@@ -69,6 +73,8 @@ def tile_routed_moe_kernel(tc, xT, w, gate, offs, pos1, pos2, out):
         weight_codes = {}
         for h in range(2):
             for e in range(E):
+                if (h, e) == (1, LAST - 1):
+                    continue
                 weight_codes[(h, e)] = keep.tile(
                     [P, PASSES * HALF], U32, name="weight_codes_%d%d" % (h, e), align_bytes=MX_ALIGN
                 )
@@ -89,8 +95,9 @@ def tile_routed_moe_kernel(tc, xT, w, gate, offs, pos1, pos2, out):
         def load_planes(g, t0, t1):
             nc.sync.dma_start(x_f32[g][:, t0:t1, :], planes[g, :, t0:t1, :])
 
-        load_planes(1, 0, 2)
         load_planes(0, 0, 1)
+        load_planes(1, 0, 1)
+        load_planes(1, 1, 2)
         load_planes(0, 1, 2)
         load_planes(1, 2, 4)
         load_planes(0, 2, 4)
@@ -184,10 +191,18 @@ def tile_routed_moe_kernel(tc, xT, w, gate, offs, pos1, pos2, out):
             nc.vector.tensor_tensor(total[:], fetched[(b, 0)][:], fetched[(b, 1)][:], mybir.AluOpType.add)
             nc.sync.dma_start(out[b * P : (b + 1) * P, :], total[:])
 
+        def finish_on_tensor(b):
+            bank = psum.tile([P, T], F32, name="sums_psum%d0" % b)
+            for r in range(2):
+                nc.tensor.matmul(out=bank[:], lhsT=identity[:], rhs=fetched[(b, r)][:], start=(r == 0), stop=(r == 1))
+            total = back.tile([P, T], F32, name="total")
+            nc.scalar.copy(out=total[:], in_=bank[:])
+            nc.sync.dma_start(out[b * P : (b + 1) * P, :], total[:])
+
         nc.vector.memset(zeros[:], 0.0)
         nc.scalar.copy(out=zeros_copy[:], in_=zeros[:])
+        make_identity(nc, identity[:])
 
-        nc.scalar.copy(out=x_bf16_1[:, 0:2, :], in_=x_f32[1][:, 0:2, :])
         for e in range(E):
             gather_on_vector(e, 0)
         nc.vector.tensor_copy(out=x_bf16_1[:, 2:4, :], in_=x_f32[1][:, 2:4, :])
@@ -195,8 +210,9 @@ def tile_routed_moe_kernel(tc, xT, w, gate, offs, pos1, pos2, out):
             gather_on_vector(e, 1)
         nc.vector.tensor_copy(out=x_bf16_0[:], in_=x_f32[0][:, 2:4, :])
 
-        for e in range(E):
-            for t in (0, 1):
+        for t in (0, 1):
+            nc.scalar.copy(out=x_bf16_1[:, t, :], in_=x_f32[1][:, t, :])
+            for e in range(E):
                 gather_on_scalar(1, e, t)
         for e in range(E):
             for t in (2, 3):
@@ -216,9 +232,10 @@ def tile_routed_moe_kernel(tc, xT, w, gate, offs, pos1, pos2, out):
                 for h in range(2):
                     interleave_weights(nc.vector.tensor_copy, h, e, g)
             if e > 0:
-                tokens_and_products(e - 1, "w_f32_%d%d" % (e, 1), range(BLOCKS))
+                tokens_and_products(e - 1, "w_f32_%d%d" % (e, 1), (0, 1))
             quantize_weights(0, e)
-            quantize_weights(1, e)
+            if e < LAST - 1:
+                quantize_weights(1, e)
         for g in range(PASSES):
             interleave_weights(nc.vector.tensor_copy, 0, LAST, g)
         tokens_and_products(LAST - 1, "w_f32_%d%d%d" % (LAST, 1, 0), (0, 1))
@@ -228,22 +245,22 @@ def tile_routed_moe_kernel(tc, xT, w, gate, offs, pos1, pos2, out):
             drain(b, 0)
         for b in (0, 1):
             drain(b, 1)
+        weight_codes[(1, LAST - 1)] = heir("tokens_bf16_1%d" % LAST, [P, PASSES * HALF], U32)
+        quantize_weights(1, LAST - 1)
+        weights_bf16[1].append(heir("tokens_bf16_0%d" % LAST, [P, PASSES, HALF, PACK], BF16))
         for g in range(PASSES):
             interleave_weights(nc.vector.tensor_copy, 1, LAST, g)
-        for b in (2, 3):
-            multiply(b, LAST - 1)
         quantize_weights(1, LAST)
         for b in (2, 3):
-            multiply(b, LAST)
-        for b in (2, 3):
-            drain(b, 0)
-        for b in (2, 3):
-            drain(b, 1)
+            for e in range(E):
+                multiply(b, e)
+                if e % 2 == 1:
+                    drain(b, e // 2)
 
-        fetch(0, 0)
-        fetch(0, 1)
-        for b in range(1, BLOCKS):
+        for b in range(BLOCKS):
             fetch(b, 0)
-            finish(b - 1)
             fetch(b, 1)
-        finish(BLOCKS - 1)
+            if b < TENSOR_SUMS:
+                finish_on_tensor(b)
+            else:
+                finish(b)

@@ -22,7 +22,7 @@ HALF = N // 2
 LIST_COLS = C // 16
 MX_ALIGN = 64
 LAST = E - 1
-TENSOR_SUMS = 3
+TENSOR_SUMS = 2
 assert TENSOR_SUMS * 2 * 2 * P * P * T <= FLOPS // 10
 
 

@@ -41,9 +41,11 @@ def tile_routed_moe_kernel(tc, xT, w, gate, offs, pos1, pos2, out):
         zeros_copy = keep.tile([P, 8], F32, name="zeros_copy")
         identity = keep.tile([P, P], F32, name="identity")
 
-        x_f32 = [keep.tile([P, PACK, T], F32, name="x_f32_%d" % g) for g in range(PASSES)]
-        x_bf16_1 = keep.tile([P, PACK, T], BF16, name="x_bf16_1")
-        x_bf16_0 = keep.tile([P, 2, T], BF16, name="x_bf16_0")
+        x_f32 = [
+            [keep.tile([P, 2, T], F32, name="x_f32_%d%d" % (g, q), align_bytes=MX_ALIGN) for q in range(2)]
+            for g in range(PASSES)
+        ]
+        x_bf16 = [keep.tile([P, PACK, T], BF16, name="x_bf16_%d" % g) for g in range(PASSES)]
 
         w_f32 = {}
         for e in range(LAST):
@@ -56,19 +58,22 @@ def tile_routed_moe_kernel(tc, xT, w, gate, offs, pos1, pos2, out):
                 )
         gate_sb = [[keep.tile([P, 2, T], F32, name="gate_sb%d%d" % (r, h)) for h in range(2)] for r in range(2)]
 
-        tokens_bf16 = [
-            [keep.tile([P, C, PACK], BF16, name="tokens_bf16_%d%d" % (g, e), align_bytes=MX_ALIGN) for e in range(E)]
+        pairs = [
+            [keep.tile([P, 2, C, 2], BF16, name="pairs_%d%d" % (g, e), align_bytes=MX_ALIGN) for e in range(E)]
             for g in range(PASSES)
         ]
+        tokens_bf16 = {}
         weights_bf16 = [
             [
                 keep.tile([P, PASSES, HALF, PACK], BF16, name="weights_bf16_%d%d" % (h, e), align_bytes=MX_ALIGN)
-                for e in range(E - h)
+                for e in range(E)
             ]
             for h in range(2)
         ]
 
-        token_codes = {}
+        token_codes = [
+            keep.tile([P, PASSES, C], U32, name="token_codes_%d" % e, align_bytes=MX_ALIGN) for e in range(E)
+        ]
         token_scales = keep.tile([P, PASSES, E * C], U8, name="token_scales", align_bytes=MX_ALIGN)
         weight_codes = {}
         for h in range(2):
@@ -84,7 +89,9 @@ def tile_routed_moe_kernel(tc, xT, w, gate, offs, pos1, pos2, out):
             [psum.tile([P, 2 * C], F32, name="sums_psum%d%d" % (b, pair)) for pair in range(E // 2)]
             for b in range(BLOCKS)
         ]
-        sums_sb = [keep.tile([P, E * C], F32, name="sums_sb%d" % b) for b in range(BLOCKS)]
+        sums_sb = {}
+        for b in (2, 3):
+            sums_sb[b] = keep.tile([P, E * C], F32, name="sums_sb%d" % b)
 
         def heir(former_name, shape, dtype):
             return keep.tile(shape, dtype, name=former_name, align_bytes=MX_ALIGN)
@@ -93,10 +100,10 @@ def tile_routed_moe_kernel(tc, xT, w, gate, offs, pos1, pos2, out):
         planes = xT.rearrange("(g p t) n -> g p t n", p=P, t=PACK)
 
         def load_planes(g, t0, t1):
-            nc.sync.dma_start(x_f32[g][:, t0:t1, :], planes[g, :, t0:t1, :])
+            nc.sync.dma_start(x_f32[g][t0 // 2][:, t0 % 2 : t0 % 2 + t1 - t0, :], planes[g, :, t0:t1, :])
 
-        load_planes(0, 0, 1)
         load_planes(1, 0, 1)
+        load_planes(0, 0, 1)
         load_planes(1, 1, 2)
         load_planes(0, 1, 2)
         load_planes(1, 2, 4)
@@ -125,20 +132,31 @@ def tile_routed_moe_kernel(tc, xT, w, gate, offs, pos1, pos2, out):
         def slots_of(e):
             return slot_token[:, e * LIST_COLS : (e + 1) * LIST_COLS]
 
+        def cast_planes(g, t0, t1):
+            nc.vector.tensor_copy(out=x_bf16[g][:, t0:t1, :], in_=x_f32[g][t0 // 2][:, t0 % 2 : t0 % 2 + t1 - t0, :])
+
         def gather_on_vector(e, t):
-            nc.vector.tensor_copy(tokens_bf16[0][e][:, :, t], x_f32[0][:, t, :].indirect(slots_of(e)))
+            nc.vector.tensor_copy(pairs[0][e][:, 0, :, t], x_f32[0][0][:, t, :].indirect(slots_of(e)))
 
         def gather_on_scalar(g, e, t):
-            window = x_bf16_1[:, t, :] if g == 1 else x_bf16_0[:, t - 2, :]
             nc.scalar.activation(
-                tokens_bf16[g][e][:, :, t], window.indirect(slots_of(e)), mybir.ActivationFunctionType.Copy
+                pairs[g][e][:, t // 2, :, t % 2],
+                x_bf16[g][:, t, :].indirect(slots_of(e)),
+                mybir.ActivationFunctionType.Copy,
+            )
+
+        def merge_pairs(g, e, former_name):
+            tokens_bf16[(g, e)] = heir(former_name, [P, C, PACK], BF16)
+            nc.vector.tensor_copy(
+                out=tokens_bf16[(g, e)][:].rearrange("p c (q w) -> p c q w", q=2),
+                in_=pairs[g][e][:].rearrange("p q c w -> p c q w"),
             )
 
         def quantize_tokens(g, e):
             nc.vector.quantize_mx(
                 out=token_codes[e][:, g, :].bitcast(FP8X4),
                 scales=token_scales[:, g, e * C : (e + 1) * C],
-                in_=tokens_bf16[g][e][:].rearrange("p c t -> p (c t)"),
+                in_=tokens_bf16[(g, e)][:].rearrange("p c t -> p (c t)"),
             )
 
         def interleave_weights(copy, h, e, g):
@@ -160,7 +178,7 @@ def tile_routed_moe_kernel(tc, xT, w, gate, offs, pos1, pos2, out):
 
         def multiply(b, e):
             h = b // 2
-            for g in range(PASSES):
+            for g in reversed(range(PASSES)):
                 first = g * HALF + (b % 2) * P
                 nc.tensor.matmul_mx(
                     out=sums_psum[b][e // 2][:, (e % 2) * C : (e % 2 + 1) * C],
@@ -168,8 +186,8 @@ def tile_routed_moe_kernel(tc, xT, w, gate, offs, pos1, pos2, out):
                     lhsT_scale=weight_scales[:, h, e, first : first + P],
                     rhs=token_codes[e][:, g, :].bitcast(FP8X4),
                     rhs_scale=token_scales[:, g, e * C : (e + 1) * C],
-                    start=(g == 0),
-                    stop=(g == PASSES - 1),
+                    start=(g == PASSES - 1),
+                    stop=(g == 0),
                 )
 
         def drain(b, pair):
@@ -203,53 +221,71 @@ def tile_routed_moe_kernel(tc, xT, w, gate, offs, pos1, pos2, out):
         nc.scalar.copy(out=zeros_copy[:], in_=zeros[:])
         make_identity(nc, identity[:])
 
+        cast_planes(1, 0, 1)
+        cast_planes(1, 1, 2)
         for e in range(E):
             gather_on_vector(e, 0)
-        nc.vector.tensor_copy(out=x_bf16_1[:, 2:4, :], in_=x_f32[1][:, 2:4, :])
+        cast_planes(1, 2, 4)
         for e in range(E):
             gather_on_vector(e, 1)
-        nc.vector.tensor_copy(out=x_bf16_0[:], in_=x_f32[0][:, 2:4, :])
-
+        cast_planes(0, 2, 4)
         for t in (0, 1):
-            nc.scalar.copy(out=x_bf16_1[:, t, :], in_=x_f32[1][:, t, :])
             for e in range(E):
                 gather_on_scalar(1, e, t)
         for e in range(E):
             for t in (2, 3):
                 gather_on_scalar(1, e, t)
+        for e in range(E):
             for t in (2, 3):
                 gather_on_scalar(0, e, t)
 
-        def tokens_and_products(e, former_name, blocks):
-            token_codes[e] = heir(former_name, [P, PASSES, C], U32)
-            quantize_tokens(1, e)
-            quantize_tokens(0, e)
-            for b in blocks:
-                multiply(b, e)
+        def tokens_of_pass(g, e, former_name):
+            merge_pairs(g, e, former_name)
+            quantize_tokens(g, e)
 
-        for e in range(LAST):
+        def weights_of(e):
             for g in range(PASSES):
                 for h in range(2):
                     interleave_weights(nc.vector.tensor_copy, h, e, g)
-            if e > 0:
-                tokens_and_products(e - 1, "w_f32_%d%d" % (e, 1), (0, 1))
-            quantize_weights(0, e)
-            if e < LAST - 1:
-                quantize_weights(1, e)
+
+        weights_of(0)
+        quantize_weights(0, 0)
+        quantize_weights(1, 0)
+        tokens_of_pass(1, 0, "w_f32_01")
+        tokens_of_pass(1, 1, "weights_bf16_00")
+        tokens_of_pass(1, 2, "weights_bf16_10")
+        weights_of(1)
+        tokens_of_pass(1, 3, "w_f32_10")
+        quantize_weights(0, 1)
+        quantize_weights(1, 1)
+        tokens_of_pass(0, 0, "w_f32_11")
+        for b in (0, 1):
+            multiply(b, 0)
+        tokens_of_pass(0, 1, "weights_bf16_01")
+        for b in (0, 1):
+            multiply(b, 1)
+        for g in range(PASSES):
+            interleave_weights(nc.vector.tensor_copy, 0, 2, g)
+            interleave_weights(nc.scalar.copy, 1, 2, g)
+        quantize_weights(0, 2)
+        tokens_of_pass(0, 2, "weights_bf16_02")
+        for b in (0, 1):
+            multiply(b, 2)
         for g in range(PASSES):
             interleave_weights(nc.vector.tensor_copy, 0, LAST, g)
-        tokens_and_products(LAST - 1, "w_f32_%d%d%d" % (LAST, 1, 0), (0, 1))
         quantize_weights(0, LAST)
-        tokens_and_products(LAST, "weights_bf16_0%d" % LAST, (0, 1))
+        tokens_of_pass(0, LAST, "weights_bf16_0%d" % LAST)
         for b in (0, 1):
+            multiply(b, LAST)
+        for b in (0, 1):
+            sums_sb[b] = heir("w_f32_2%d" % b, [P, E * C], F32)
             drain(b, 0)
+        interleave_weights(nc.scalar.copy, 1, LAST, 0)
         for b in (0, 1):
             drain(b, 1)
-        weight_codes[(1, LAST - 1)] = heir("tokens_bf16_1%d" % LAST, [P, PASSES * HALF], U32)
+        weight_codes[(1, LAST - 1)] = heir("pairs_0%d" % LAST, [P, PASSES * HALF], U32)
         quantize_weights(1, LAST - 1)
-        weights_bf16[1].append(heir("tokens_bf16_0%d" % LAST, [P, PASSES, HALF, PACK], BF16))
-        for g in range(PASSES):
-            interleave_weights(nc.vector.tensor_copy, 1, LAST, g)
+        interleave_weights(nc.vector.tensor_copy, 1, LAST, 1)
         quantize_weights(1, LAST)
         for b in (2, 3):
             for e in range(E):

@@ -78,7 +78,7 @@ def tile_routed_moe_kernel(tc, xT, w, gate, offs, pos1, pos2, out):
         weight_codes = {}
         for h in range(2):
             for e in range(E):
-                if (h, e) == (1, LAST - 1):
+                if h == 1 and e in (1, 2):
                     continue
                 weight_codes[(h, e)] = keep.tile(
                     [P, PASSES * HALF], U32, name="weight_codes_%d%d" % (h, e), align_bytes=MX_ALIGN
@@ -248,44 +248,58 @@ def tile_routed_moe_kernel(tc, xT, w, gate, offs, pos1, pos2, out):
                 for h in range(2):
                     interleave_weights(nc.vector.tensor_copy, h, e, g)
 
+        V = nc.vector.tensor_copy
+        S = nc.scalar.copy
         weights_of(0)
         quantize_weights(0, 0)
         quantize_weights(1, 0)
-        tokens_of_pass(1, 0, "w_f32_01")
-        tokens_of_pass(1, 1, "weights_bf16_00")
-        tokens_of_pass(1, 2, "weights_bf16_10")
-        weights_of(1)
-        tokens_of_pass(1, 3, "w_f32_10")
+        merge_pairs(1, 0, "w_f32_01")
+        merge_pairs(1, 1, "weights_bf16_00")
+        quantize_tokens(1, 0)
+        merge_pairs(1, 2, "weights_bf16_10")
+        quantize_tokens(1, 1)
+        merge_pairs(1, 3, "w_f32_01")
+        quantize_tokens(1, 2)
+        interleave_weights(V, 0, 1, 0)
+        quantize_tokens(1, 3)
+        interleave_weights(V, 0, 1, 1)
         quantize_weights(0, 1)
-        quantize_weights(1, 1)
-        tokens_of_pass(0, 0, "w_f32_11")
+        for e in (1, 2):
+            for g in range(PASSES):
+                interleave_weights(S, 1, e, g)
+        merge_pairs(0, 0, "weights_bf16_00")
+        merge_pairs(0, 1, "w_f32_01")
+        quantize_tokens(0, 0)
         for b in (0, 1):
             multiply(b, 0)
-        tokens_of_pass(0, 1, "weights_bf16_01")
+        merge_pairs(0, 2, "weights_bf16_01")
+        quantize_tokens(0, 1)
         for b in (0, 1):
             multiply(b, 1)
-        for g in range(PASSES):
-            interleave_weights(nc.vector.tensor_copy, 0, 2, g)
-            interleave_weights(nc.scalar.copy, 1, 2, g)
+        quantize_tokens(0, 2)
+        interleave_weights(V, 0, 2, 0)
+        interleave_weights(V, 0, 2, 1)
         quantize_weights(0, 2)
-        tokens_of_pass(0, 2, "weights_bf16_02")
         for b in (0, 1):
             multiply(b, 2)
-        for g in range(PASSES):
-            interleave_weights(nc.vector.tensor_copy, 0, LAST, g)
+        merge_pairs(0, LAST, "weights_bf16_02")
+        interleave_weights(V, 0, LAST, 0)
+        quantize_tokens(0, LAST)
+        interleave_weights(V, 0, LAST, 1)
         quantize_weights(0, LAST)
-        tokens_of_pass(0, LAST, "weights_bf16_0%d" % LAST)
         for b in (0, 1):
             multiply(b, LAST)
         for b in (0, 1):
             sums_sb[b] = heir("w_f32_2%d" % b, [P, E * C], F32)
             drain(b, 0)
-        interleave_weights(nc.scalar.copy, 1, LAST, 0)
         for b in (0, 1):
             drain(b, 1)
-        weight_codes[(1, LAST - 1)] = heir("pairs_0%d" % LAST, [P, PASSES * HALF], U32)
-        quantize_weights(1, LAST - 1)
-        interleave_weights(nc.vector.tensor_copy, 1, LAST, 1)
+        weight_codes[(1, 1)] = heir("weights_bf16_0%d" % LAST, [P, PASSES * HALF], U32)
+        quantize_weights(1, 1)
+        for g in range(PASSES):
+            interleave_weights(V, 1, LAST, g)
+        weight_codes[(1, 2)] = heir("w_f32_%d%d%d" % (LAST, 1, 0), [P, PASSES * HALF], U32)
+        quantize_weights(1, 2)
         quantize_weights(1, LAST)
         for b in (2, 3):
             for e in range(E):

@@ -263,12 +263,12 @@ def tile_routed_moe_kernel(tc, xT, w, gate, offs, pos1, pos2, out):
         interleave_weights(V, 0, 1, 0)
         quantize_tokens(1, 3)
         interleave_weights(V, 0, 1, 1)
-        quantize_weights(0, 1)
         for e in (1, 2):
             for g in range(PASSES):
                 interleave_weights(S, 1, e, g)
         merge_pairs(0, 0, "weights_bf16_00")
         merge_pairs(0, 1, "w_f32_01")
+        quantize_weights(0, 1)
         quantize_tokens(0, 0)
         for b in (0, 1):
             multiply(b, 0)
@@ -279,10 +279,10 @@ def tile_routed_moe_kernel(tc, xT, w, gate, offs, pos1, pos2, out):
         quantize_tokens(0, 2)
         interleave_weights(V, 0, 2, 0)
         interleave_weights(V, 0, 2, 1)
+        merge_pairs(0, LAST, "w_f32_01")
         quantize_weights(0, 2)
         for b in (0, 1):
             multiply(b, 2)
-        merge_pairs(0, LAST, "weights_bf16_02")
         interleave_weights(V, 0, LAST, 0)
         quantize_tokens(0, LAST)
         interleave_weights(V, 0, LAST, 1)
@@ -294,10 +294,10 @@ def tile_routed_moe_kernel(tc, xT, w, gate, offs, pos1, pos2, out):
             drain(b, 0)
         for b in (0, 1):
             drain(b, 1)
+        interleave_weights(V, 1, LAST, 0)
         weight_codes[(1, 1)] = heir("weights_bf16_0%d" % LAST, [P, PASSES * HALF], U32)
         quantize_weights(1, 1)
-        for g in range(PASSES):
-            interleave_weights(V, 1, LAST, g)
+        interleave_weights(V, 1, LAST, 1)
         weight_codes[(1, 2)] = heir("w_f32_%d%d%d" % (LAST, 1, 0), [P, PASSES * HALF], U32)
         quantize_weights(1, 2)
         quantize_weights(1, LAST)
@@ -307,10 +307,13 @@ def tile_routed_moe_kernel(tc, xT, w, gate, offs, pos1, pos2, out):
                 if e % 2 == 1:
                     drain(b, e // 2)
 
-        for b in range(BLOCKS):
+        for b in range(TENSOR_SUMS):
             fetch(b, 0)
             fetch(b, 1)
-            if b < TENSOR_SUMS:
-                finish_on_tensor(b)
-            else:
-                finish(b)
+            finish_on_tensor(b)
+        fetch(2, 0)
+        fetch(2, 1)
+        fetch(3, 0)
+        finish(2)
+        fetch(3, 1)
+        finish(3)

from contextlib import ExitStack

import concourse.mybir as mybir
from concourse.masks import make_identity

K, T, E, C, N = 1024, 512, 4, 256, 512
FLOPS = 2 * K * N * E * C

F32 = mybir.dt.float32
BF16 = mybir.dt.bfloat16
U32 = mybir.dt.uint32
U16 = mybir.dt.uint16
U8 = mybir.dt.uint8
FP8X4 = mybir.dt.float8_e4m3fn_x4

P = 128
PACK = 4
K_PASS = P * PACK
PASSES = K // K_PASS
BLOCKS = N // P
HALF = N // 2
LIST_COLS = C // 16
MX_ALIGN = 64
LAST = E - 1
TENSOR_SUMS = 2
assert TENSOR_SUMS * 2 * 2 * P * P * T <= FLOPS // 10


def tile_routed_moe_kernel(tc, xT, w, gate, offs, pos1, pos2, out):
    nc = tc.nc
    with ExitStack() as ctx:
        lists = ctx.enter_context(tc.tile_pool(name="lists", bufs=1))
        keep = ctx.enter_context(tc.tile_pool(name="keep", bufs=1))
        back = ctx.enter_context(tc.tile_pool(name="back", bufs=3))
        psum = ctx.enter_context(tc.psum_pool(name="psum", bufs=1))

        slot_token = lists.tile([P, E * C // 16], U16, name="slot_token")
        token_slot = [lists.tile([P, T // 16], U16, name="token_slot%d" % r) for r in range(2)]

        zeros = keep.tile([P, 8], F32, name="zeros")
        zeros_copy = keep.tile([P, 8], F32, name="zeros_copy")
        identity = keep.tile([P, P], F32, name="identity")

        x_f32 = [
            [keep.tile([P, 2, T], F32, name="x_f32_%d%d" % (g, q), align_bytes=MX_ALIGN) for q in range(2)]
            for g in range(PASSES)
        ]
        x_bf16 = [keep.tile([P, PACK, T], BF16, name="x_bf16_%d" % g) for g in range(PASSES)]

        w_f32 = {}
        for e in range(LAST):
            for g in range(PASSES):
                w_f32[(e, g)] = keep.tile([P, PACK, N], F32, name="w_f32_%d%d" % (e, g), align_bytes=MX_ALIGN)
        for h in range(2):
            for g in range(PASSES):
                w_f32[(LAST, g, h)] = keep.tile(
                    [P, PACK, HALF], F32, name="w_f32_%d%d%d" % (LAST, g, h), align_bytes=MX_ALIGN
                )
        gate_sb = [[keep.tile([P, 2, T], F32, name="gate_sb%d%d" % (r, h)) for h in range(2)] for r in range(2)]

        pairs = [
            [keep.tile([P, 2, C, 2], BF16, name="pairs_%d%d" % (g, e), align_bytes=MX_ALIGN) for e in range(E)]
            for g in range(PASSES)
        ]
        tokens_bf16 = {}
        weights_bf16 = [
            [
                keep.tile([P, PASSES, HALF, PACK], BF16, name="weights_bf16_%d%d" % (h, e), align_bytes=MX_ALIGN)
                for e in range(E)
            ]
            for h in range(2)
        ]

        token_codes = [
            keep.tile([P, PASSES, C], U32, name="token_codes_%d" % e, align_bytes=MX_ALIGN) for e in range(E)
        ]
        token_scales = keep.tile([P, PASSES, E * C], U8, name="token_scales", align_bytes=MX_ALIGN)
        weight_codes = {}
        for h in range(2):
            for e in range(E):
                if h == 1 and e in (1, 2):
                    continue
                weight_codes[(h, e)] = keep.tile(
                    [P, PASSES * HALF], U32, name="weight_codes_%d%d" % (h, e), align_bytes=MX_ALIGN
                )
        weight_scales = keep.tile([P, 2, E, PASSES * HALF], U8, name="weight_scales", align_bytes=MX_ALIGN)

        sums_psum = [
            [psum.tile([P, 2 * C], F32, name="sums_psum%d%d" % (b, pair)) for pair in range(E // 2)]
            for b in range(BLOCKS)
        ]
        sums_sb = {}
        for b in (2, 3):
            sums_sb[b] = keep.tile([P, E * C], F32, name="sums_sb%d" % b)

        def heir(former_name, shape, dtype):
            return keep.tile(shape, dtype, name=former_name, align_bytes=MX_ALIGN)

        nc.sync.dma_start(slot_token[:], offs)
        planes = xT.rearrange("(g p t) n -> g p t n", p=P, t=PACK)

        def load_planes(g, t0, t1):
            nc.sync.dma_start(x_f32[g][t0 // 2][:, t0 % 2 : t0 % 2 + t1 - t0, :], planes[g, :, t0:t1, :])

        load_planes(1, 0, 1)
        load_planes(0, 0, 1)
        load_planes(1, 1, 2)
        load_planes(0, 1, 2)
        load_planes(1, 2, 4)
        load_planes(0, 2, 4)
        for e in range(LAST):
            for g in range(PASSES):
                nc.sync.dma_start(
                    w_f32[(e, g)][:], w[e, g * K_PASS : (g + 1) * K_PASS, :].rearrange("(p j) n -> p j n", j=PACK)
                )
        for h in range(2):
            for g in range(PASSES):
                nc.sync.dma_start(
                    w_f32[(LAST, g, h)][:],
                    w[LAST, g * K_PASS : (g + 1) * K_PASS, h * HALF : (h + 1) * HALF].rearrange(
                        "(p j) n -> p j n", j=PACK
                    ),
                )
        nc.sync.dma_start(token_slot[0][:], pos1)
        nc.sync.dma_start(token_slot[1][:], pos2)
        for h in range(2):
            for r in range(2):
                nc.sync.dma_start(
                    gate_sb[r][h][:], gate[r, h * HALF : (h + 1) * HALF, :].rearrange("(b p) t -> p b t", p=P)
                )

        def slots_of(e):
            return slot_token[:, e * LIST_COLS : (e + 1) * LIST_COLS]

        def cast_planes(g, t0, t1):
            nc.vector.tensor_copy(out=x_bf16[g][:, t0:t1, :], in_=x_f32[g][t0 // 2][:, t0 % 2 : t0 % 2 + t1 - t0, :])

        def gather_on_vector(e, t):
            nc.vector.tensor_copy(pairs[0][e][:, 0, :, t], x_f32[0][0][:, t, :].indirect(slots_of(e)))

        def gather_on_scalar(g, e, t):
            nc.scalar.activation(
                pairs[g][e][:, t // 2, :, t % 2],
                x_bf16[g][:, t, :].indirect(slots_of(e)),
                mybir.ActivationFunctionType.Copy,
            )

        def merge_pairs(g, e, former_name):
            tokens_bf16[(g, e)] = heir(former_name, [P, C, PACK], BF16)
            nc.vector.tensor_copy(
                out=tokens_bf16[(g, e)][:].rearrange("p c (q w) -> p c q w", q=2),
                in_=pairs[g][e][:].rearrange("p q c w -> p c q w"),
            )

        def quantize_tokens(g, e):
            nc.vector.quantize_mx(
                out=token_codes[e][:, g, :].bitcast(FP8X4),
                scales=token_scales[:, g, e * C : (e + 1) * C],
                in_=tokens_bf16[(g, e)][:].rearrange("p c t -> p (c t)"),
            )

        def interleave_weights(copy, h, e, g):
            if e == LAST:
                rows = w_f32[(e, g, h)][:]
            else:
                rows = w_f32[(e, g)][:, :, h * HALF : (h + 1) * HALF]
            copy(
                out=weights_bf16[h][e][:, g, :, :].rearrange("p (c i) t -> p c t i", i=4),
                in_=rows.rearrange("p t (c i) -> p c t i", i=4),
            )

        def quantize_weights(h, e):
            nc.vector.quantize_mx(
                out=weight_codes[(h, e)][:].bitcast(FP8X4),
                scales=weight_scales[:, h, e, :],
                in_=weights_bf16[h][e][:].rearrange("p g c t -> p (g c t)"),
            )

        def multiply(b, e):
            h = b // 2
            for g in reversed(range(PASSES)):
                first = g * HALF + (b % 2) * P
                nc.tensor.matmul_mx(
                    out=sums_psum[b][e // 2][:, (e % 2) * C : (e % 2 + 1) * C],
                    lhsT=weight_codes[(h, e)][:, first : first + P].bitcast(FP8X4),
                    lhsT_scale=weight_scales[:, h, e, first : first + P],
                    rhs=token_codes[e][:, g, :].bitcast(FP8X4),
                    rhs_scale=token_scales[:, g, e * C : (e + 1) * C],
                    start=(g == PASSES - 1),
                    stop=(g == 0),
                )

        def drain(b, pair):
            nc.scalar.copy(out=sums_sb[b][:, pair * 2 * C : (pair + 1) * 2 * C], in_=sums_psum[b][pair][:])

        fetched = {}

        def fetch(b, r):
            fetched[(b, r)] = back.tile([P, T], F32, name="fetched%d" % r)
            nc.vector.tensor_tensor(
                fetched[(b, r)][:],
                sums_sb[b][:].indirect(token_slot[r][:]),
                gate_sb[r][b // 2][:, b % 2, :],
                mybir.AluOpType.mult,
            )

        def finish(b):
            total = back.tile([P, T], F32, name="total")
            nc.vector.tensor_tensor(total[:], fetched[(b, 0)][:], fetched[(b, 1)][:], mybir.AluOpType.add)
            nc.sync.dma_start(out[b * P : (b + 1) * P, :], total[:])

        def finish_on_tensor(b):
            bank = psum.tile([P, T], F32, name="sums_psum%d0" % b)
            for r in range(2):
                nc.tensor.matmul(out=bank[:], lhsT=identity[:], rhs=fetched[(b, r)][:], start=(r == 0), stop=(r == 1))
            total = back.tile([P, T], F32, name="total")
            nc.scalar.copy(out=total[:], in_=bank[:])
            nc.sync.dma_start(out[b * P : (b + 1) * P, :], total[:])

        nc.vector.memset(zeros[:], 0.0)
        nc.scalar.copy(out=zeros_copy[:], in_=zeros[:])
        make_identity(nc, identity[:])

        cast_planes(1, 0, 1)
        cast_planes(1, 1, 2)
        for e in range(E):
            gather_on_vector(e, 0)
        cast_planes(1, 2, 4)
        for e in range(E):
            gather_on_vector(e, 1)
        cast_planes(0, 2, 4)
        for t in (0, 1):
            for e in range(E):
                gather_on_scalar(1, e, t)
        for e in range(E):
            for t in (2, 3):
                gather_on_scalar(1, e, t)
        for e in range(E):
            for t in (2, 3):
                gather_on_scalar(0, e, t)

        def tokens_of_pass(g, e, former_name):
            merge_pairs(g, e, former_name)
            quantize_tokens(g, e)

        def weights_of(e):
            for g in range(PASSES):
                for h in range(2):
                    interleave_weights(nc.vector.tensor_copy, h, e, g)

        V = nc.vector.tensor_copy
        S = nc.scalar.copy
        weights_of(0)
        quantize_weights(0, 0)
        quantize_weights(1, 0)
        merge_pairs(1, 0, "w_f32_01")
        merge_pairs(1, 1, "weights_bf16_00")
        quantize_tokens(1, 0)
        merge_pairs(1, 2, "weights_bf16_10")
        quantize_tokens(1, 1)
        merge_pairs(1, 3, "w_f32_01")
        quantize_tokens(1, 2)
        interleave_weights(V, 0, 1, 0)
        quantize_tokens(1, 3)
        interleave_weights(V, 0, 1, 1)
        for e in (1, 2):
            for g in range(PASSES):
                interleave_weights(S, 1, e, g)
        merge_pairs(0, 0, "weights_bf16_00")
        merge_pairs(0, 1, "w_f32_01")
        quantize_weights(0, 1)
        quantize_tokens(0, 0)
        for b in (0, 1):
            multiply(b, 0)
        merge_pairs(0, 2, "weights_bf16_01")
        quantize_tokens(0, 1)
        for b in (0, 1):
            multiply(b, 1)
        quantize_tokens(0, 2)
        interleave_weights(V, 0, 2, 0)
        interleave_weights(V, 0, 2, 1)
        merge_pairs(0, LAST, "w_f32_01")
        quantize_weights(0, 2)
        for b in (0, 1):
            multiply(b, 2)
        interleave_weights(V, 0, LAST, 0)
        quantize_tokens(0, LAST)
        interleave_weights(V, 0, LAST, 1)
        quantize_weights(0, LAST)
        for b in (0, 1):
            multiply(b, LAST)
        for b in (0, 1):
            sums_sb[b] = heir("w_f32_2%d" % b, [P, E * C], F32)
            drain(b, 0)
        for b in (0, 1):
            drain(b, 1)
        interleave_weights(V, 1, LAST, 0)
        weight_codes[(1, 1)] = heir("weights_bf16_0%d" % LAST, [P, PASSES * HALF], U32)
        quantize_weights(1, 1)
        interleave_weights(V, 1, LAST, 1)
        weight_codes[(1, 2)] = heir("w_f32_%d%d%d" % (LAST, 1, 0), [P, PASSES * HALF], U32)
        quantize_weights(1, 2)
        quantize_weights(1, LAST)
        for b in (2, 3):
            for e in range(E):
                multiply(b, e)
                if e % 2 == 1:
                    drain(b, e // 2)

        for b in range(TENSOR_SUMS):
            fetch(b, 0)
            fetch(b, 1)
            finish_on_tensor(b)
        fetch(2, 0)
        fetch(2, 1)
        fetch(3, 0)
        finish(2)
        fetch(3, 1)
        finish(3)
